import numpy as np, ml_dtypes
CORES = [8,136,40,168]
N = 4
BF = ml_dtypes.bfloat16
S, R, B, CAP = 512, 128, 4, 288
L, IT, I = 4, 4, 16
D, TOP, F = 2, 2, 1
def where_to(rep):
    i = np.arange(N * S); first = np.maximum.accumulate(np.where(rep == 0, i, 0)); rec = np.add.accumulate((rep == 0).astype(np.int64)) - 1
    kth = np.add.accumulate((rep == 1).astype(np.int64)); head = np.maximum.accumulate(np.where(rep < 2, i, 0))
    return rec, kth - kth[first], i - head
def count(rec):
    return np.bincount(np.arange(N * S) // S * N + rec // B % N, minlength=N * N)
def parts(rng, lens, total):
    diff = int(total - np.sum(lens)); room = I - lens if diff > 0 else lens - 1
    k = np.bincount(rng.permutation(np.repeat(np.arange(len(lens)), room))[:abs(diff)], minlength=len(lens))
    return lens + (k if diff > 0 else -k)
def rich(rng, n, total):
    return parts(rng, np.where(rng.random(n) * ((I - 1) * n) < 2 * (total - n), rng.integers(1, I + 1, n), 1), total)
def levels(rng, lens):
    if count(np.repeat(np.arange(len(lens)), lens)).max() > CAP:
        lens = np.diff(np.arange(N * R + 1) * (N * S) // (N * R))
    rep = np.full(N * S, TOP, np.int32); rep[np.add.accumulate(lens) - lens] = 0
    if L > 1:
        u = rng.random(N * S).tolist(); i = 0
        for n in lens.tolist():
            k = c = 1
            for j in range(1, n):
                if c == IT or (k < L and n - j <= (L - k) * IT and u[i + j] < 0.35):
                    rep[i + j] = 1; k += 1; c = 1
                else: c += 1
            i += n
    return rep
def values(rng):
    return rng.integers(0, 1 << 20, (N, 8, S)).astype(np.int32)
def make(rng, cols, p):
    rl = np.ascontiguousarray(np.stack([levels(rng, c) for c in cols]).reshape(8, N, S).transpose(1, 0, 2))
    dl = np.where(rng.random((N, 8, S)) < p, D, rng.integers(0, D, (N, 8, S))).astype(np.int32)
    return {"rl": rl, "dl": dl, "val": values(rng)}
def setup_inputs(rng):
    cols = [rich(rng, int(rng.integers(N * R * 3 // 4, N * R + 1)), N * S) for g in range(8)]
    return make(rng, cols, rng.integers(4, 16, (N, 8, 1)) * 0.0625)
def setup_inputs_full(rng):
    cols = []; mix = rng.permutation(8).tolist(); odd = mix[:4]; home = mix[4]; m = R // N
    for g in range(8):
        if g in odd: cols.append(rich(rng, N * R, N * S)); continue
        c = []
        for q in range(N):
            d = q if g == home else (q + 1 + g % (N - 1)) % N; own = np.arange(R) // B % N == d; v = np.ones(R, np.int64)
            v[own] = parts(rng, v[own], CAP); v[~own] = parts(rng, v[~own], S - CAP); c.append(v)
        cols.append(np.concatenate(c))
    return make(rng, cols, rng.choice(np.array([0.5, 1.0]), (N, 8, 1)))
def setup_inputs_edges(rng):
    cols = []
    for g in range(8):
        a = rng.integers(0, I + 1, N - 1); c = []; at = 0
        if g < 4: a[:] = (0, I, 1, I - 1)[g]
        for q in range(1, N + 1):
            end = q * S - int(a[q - 1]) if q < N else N * S; seg = end - at
            c.append(rich(rng, max(-(-seg // I), seg * R * int(rng.integers(12, 17)) // (16 * S)), seg))
            if q < N: c.append(np.array([I])); at = end + I
        cols.append(np.concatenate(c))
    return make(rng, cols, rng.integers(0, 3, (N, 8, 1)) * 0.5)
def setup_inputs_few(rng):
    cols = []
    for g in range(8):
        h = int(rng.integers(1, I + 1)) if g else I; k = (N * S - h) // I; t = N * S - h - k * I
        cols.append(np.array([h] + [I] * k + ([t] if t else [])))
    p = rng.integers(8, 17, (N, 8, 1)) * 0.0625; p[:, rng.integers(0, 8)] = 0
    return make(rng, cols, p)
def setup_inputs_spread(rng):
    cols = [rich(rng, int(rng.integers(N * S // I, N * R + 1)), N * S) for g in range(8)]
    d = make(rng, cols, rng.integers(1, 16, (N, 8, 1)) * 0.0625)
    v = d["val"] >> rng.integers(0, 21, (N, 8, S)); d["val"] = np.where(rng.random((N, 8, S)) < 0.0625, (1 << 20) - 1, v).astype(np.int32)
    return d
def check_inputs(d):
    rl, dl, val = d["rl"], d["dl"], d["val"]; bad = []
    if not (((rl >= 0) & (rl <= TOP)).all() and ((dl >= 0) & (dl <= D)).all()): bad.append("levels")
    if not (rl[0, :, 0] == 0).all(): bad.append("first")
    if not (((val >= 0) & (val < 1 << 20)).all()): bad.append("values")
    if bad: return bad
    for g in range(8):
        rec, lst, item = where_to(rl[:, g].reshape(-1))
        if rec[-1] >= N * R: bad.append("records")
        if lst.max() >= L or item.max() >= IT: bad.append("items")
        if count(rec).max() > CAP: bad.append("pairs")
    return sorted(set(bad))
def reference(rl, dl, val):
    y = np.full((N, 8, F, R * I), -2, np.float32); x = val.reshape(N, 8, F, S); q = np.arange(N * S) // S
    for g in range(8):
        rec, lst, item = where_to(rl[:, g].reshape(-1)); lev = dl[:, g].reshape(-1)
        has = (dl[:, g] == D).astype(np.int64); v = (np.add.accumulate(has, axis=1) - has).reshape(-1)
        e = np.where((lev == D)[:, None], x[q, g, :, v].astype(np.float32), (lev - D)[:, None])
        y[rec // B % N, g, :, (rec // (B * N) * B + rec % B) * I + lst * IT + item] = e
    return {"y": y.reshape(N, 8 * F, R * I).astype(np.float32)}

@@ -1,0 +1,245 @@
+from concourse.bass import DstId, RemoteDMATransfer
+from concourse.mybir import AluOpType as A, ActivationFunctionType as F
+
+H = 26
+BLK, COLS = 4 * H, 16 * H
+WINW = 17 * COLS
+VWW = 16 + 512
+I32, F32, B16, U16 = "int32", "float32", "bfloat16", "uint16"
+
+
+def sb(width, dtype):
+    return ("sbuf", [128] + (width if isinstance(width, list) else [width]), dtype)
+
+
+SCRATCH = {
+    "lt0": sb(64, I32), "lw": sb(64, I32), "rlc": sb(144, I32), "vw": sb(VWW, I32),
+    "ff": sb(65, B16), "sm": sb(65, B16), "f2": sb(32, B16), "s2": sb(32, B16),
+    "mn": sb(32, F32), "offv": sb(32, U16), "offs": sb(32, U16), "hh": sb(32, B16),
+    "ca": sb(144, B16), "cb": sb(144, B16), "cp": sb(144, B16), "rst": sb(144, B16),
+    "ha": sb(48, B16), "hb": sb(48, B16), "hp": sb(48, B16),
+    "mask": sb(512, B16), "maskh": sb(32, B16), "mm": sb(512, F32), "vv": sb(512, F32), "win": sb(WINW, F32),
+    "msg0": sb(32, B16), "msg1": sb(32, B16), "msg2": sb(32, B16),
+    "from0": sb([4, H], F32), "from1": sb([4, H], F32), "from2": sb([4, H], F32), "from3": sb([4, H], F32),
+    "acc": sb([4, 32], F32), "ta": sb([4, 32], F32), "fin": sb([2, 4, 16], F32),
+    "mg": sb(128, B16), "mi": sb(128, B16), "sg": sb(128, B16), "lt": sb(128, B16), "idn": sb(128, B16), "idh": sb(128, B16),
+    "sel0": sb(128, B16), "sel1": sb(128, B16), "sel2": sb(128, B16), "sel3": sb(128, B16),
+    "sgv": sb(128, B16), "lvv": sb(128, B16), "sgr": sb(128, B16), "ltr": sb(128, B16),
+    "d1s": sb(128, B16), "d2s": sb(128, B16),
+    "pi": sb(1, I32), "pa": sb(1, I32), "kg": sb(1, I32), "pif": sb(1, F32), "paf": sb(1, F32), "kgf": sb(1, F32),
+    "kmod": sb(1, F32), "pm1": sb(1, F32), "p15": sb(1, F32), "zc": sb(1, F32),
+    "ccol": sb(1, F32), "mb": sb(1, F32), "pcol": sb(1, F32), "kcol": sb(1, F32),
+}
+for _b in ("ps1", "ps2", "psv", "psh", "psw0", "psw1", "psr"):
+    SCRATCH[_b] = ("psum", [128, 512], "float32")
+SEMAPHORES = ["s%d" % i for i in range(110)] + ["m0", "m1", "m2", "t", "h0", "h1", "h2", "h3", "loc0", "loc1", "loc2"]
+
+
+def rank_program(g, core, T, topo):
+    r = T.rank_of(core)
+    if r is None:
+        return
+    N = len(T.cores)
+    queues = {"g": g, "v": g.vector, "s": g.scalar, "p": g.tensor, "y": g.sync}
+    seen = {q: [] for q in queues}
+    used = []
+
+    def after(q, deps):
+        for d in deps:
+            if d not in seen[q]:
+                queues[q].wait_ge(T.sem[d[0]], d[1])
+                seen[q].append(d)
+
+    def new():
+        used.append("s%d" % len(used))
+        return used[-1]
+
+    def do(q, call, deps=()):
+        after(q, deps)
+        n = new()
+        call(queues[q]).then_inc(T.sem[n], 1)
+        return (n, 1)
+
+    def load(parts):
+        n = new()
+        for q, out, in_ in parts:
+            queues[q].dma_start(out, in_).then_inc(T.sem[n], 16)
+        return (n, 16 * len(parts))
+
+    def ts(out, in0, s1, op0, s2=None, op1=None, deps=()):
+        if op1 is None:
+            return do("v", lambda e: e.tensor_scalar(out, in0, s1, None, op0), deps)
+        return do("v", lambda e: e.tensor_scalar(out, in0, s1, s2, op0, op1), deps)
+
+    def scan(out, x0, x1, initial, op0, op1, deps=()):
+        return do("v", lambda e: e.tensor_tensor_scan(out, x0, x1, initial, op0, op1), deps)
+
+    def tt(out, in0, in1, op, deps=()):
+        return do("v", lambda e: e.tensor_tensor(out, in0, in1, op), deps)
+
+    def mat(out, lhs, rhs, start, stop, deps=()):
+        return do("p", lambda e: e.matmul(out, lhs, rhs, start, stop), deps)
+
+    def act(out, in_, func, bias=0.0, scale=1.0, deps=()):
+        return do("s", lambda e: e.activation(out, in_, func, bias=bias, scale=scale), deps)
+
+    blk = [(a - r) % 4 for a in range(4)]
+    later = [d for d in range(r + 1, N)]
+
+    parts = []
+    for a in range(4):
+        for q, row in (("y", 8 * blk[a]), ("s", 32 + 8 * blk[a])):
+            lo = max(0, 128 * a - 16)
+            parts.append((q, T.rlc[row:row + 8, :], T.rl[:, lo:lo + 144]))
+    l_rlc = load(parts)
+    l_lst = load([("y", T.lt0[:, 0:16], T.rl[0::2, :]), ("s", T.lt0[:, 16:32], T.rl[1::2, :]),
+                  ("y", T.lt0[:, 32:48], T.dl[0::2, :]), ("s", T.lt0[:, 48:64], T.dl[1::2, :])])
+
+    pi = do("g", lambda e: e.iota(T.pi[:, :], [[0, 1]], 0, 1))
+    mg = do("g", lambda e: e.iota(T.mg[:, :], [[1, 8], [0, 16]], 0, 0, allow_small_or_imprecise_dtypes=True))
+    mi = do("g", lambda e: e.iota(T.mi[:, :], [[1, 128]], 0, 0, allow_small_or_imprecise_dtypes=True))
+    cc = [do("v", lambda e: e.memset(T.ccol[32 * i:32 * i + 32, :], 8.0 + i)) for i in range(2)]
+    fz = do("v", lambda e: e.memset(T.ff[:, 33:65], 0.0))
+    f1 = do("v", lambda e: e.memset(T.ff[:, 32:33], 1.0))
+    tz = do("v", lambda e: e.memset(T.ca[64:128, 128:144], 0.0)) if later else None
+    vn = [do("v", lambda e: e.memset(T.vw[:, 0:4], -2)), do("v", lambda e: e.memset(T.vw[:, 4:16], -1))]
+    pif = do("v", lambda e: e.tensor_copy(T.pif[:, :], T.pi[:, :]), [pi])
+    kg = ts(T.kg[:, :], T.pi[:, :], 4, A.arith_shift_right)
+    pa = ts(T.pa[:, :], T.pi[:, :], 15, A.bitwise_and)
+    kgf = do("v", lambda e: e.tensor_copy(T.kgf[:, :], T.kg[:, :]), [kg])
+    paf = do("v", lambda e: e.tensor_copy(T.paf[:, :], T.pa[:, :]), [pa])
+    sg = ts(T.sg[:, :], T.mg[:, :], T.kgf[:, :], A.is_equal, deps=[mg, kgf])
+    lt = do("g", lambda e: e.affine_select(T.lt[:, :], T.sg[:, :], [[-1, 128]], A.is_ge, 0.0, -1, 1), [sg])
+    km = [act(T.kmod[32 * i:32 * i + 32, :], T.pif[32 * i:32 * i + 32, :], F.Copy, bias=-32.0 * i, deps=[pif]) for i in range(2)]
+    l_val = load([("sy"[w > 5], T.vw[w::16, 16:528], T.val[:, :]) for w in range(16)])
+    zc = ts(T.zc[:, :], T.paf[:, :], 0.0, A.is_equal, -16.0 * COLS, A.mult, [paf])
+    sel = [ts(T["sel%d" % a][0:64, :], T.mg[0:64, :], 8.0 * blk[a], A.add, T.kmod[0:64, :], A.is_equal, km) for a in range(4)]
+
+    mb = act(T.mb[:, :], T.paf[:, :], F.Copy, scale=-2048.0, deps=[paf])
+    kcol = act(T.kcol[:, :], T.paf[:, :], F.Copy, scale=-float(COLS))
+    pm1 = act(T.pm1[:, :], T.pif[:, :], F.Copy, bias=-1.0)
+    p15 = act(T.p15[:, :], T.pif[:, :], F.Copy, bias=15.0)
+    sgv = act(T.sgv[:, :], T.sg[:, :], F.Copy, scale=1.0 / 1024, deps=[sg])
+    lvv = act(T.lvv[:, :], T.lt[:, :], F.Copy, scale=-1.0 / 1024, deps=[lt])
+
+    ca = ts(T.ca[0:64, :], T.rlc[0:64, :], -4.0, A.mult, T.ccol[0:64, :], A.add, [l_rlc] + cc)
+    lw = do("v", lambda e: e.transpose(T.lw[:, :], T.lt0[:, :]), [l_lst])
+    cb = ts(T.cb[0:64, :], T.ca[0:64, :], 4.5, A.is_le, 16.0, A.mult, [ca])
+    f0 = ts(T.ff[:, 0:32], T.lw[:, 0:32], 0.0, A.is_equal, deps=[lw])
+    cp = scan(T.cp[0:64, :], T.ca[0:64, :], T.cb[0:64, :], 0.0, A.add, A.min, [cb])
+    sm = scan(T.sm[:, :], T.ff[:, :], T.ff[:, :], 0.0, A.add, A.max, [f0, f1, fz])
+    f2 = ts(T.f2[:, :], T.lw[:, 32:64], 2.0, A.is_equal)
+    s2 = scan(T.s2[:, :], T.f2[:, :], T.f2[:, :], 64.5, A.add, A.max, [f2])
+    idn = ts(T.idn[:, :], T.mi[:, :], T.pif[:, :], A.is_equal, deps=[mi])
+    idh = ts(T.idh[:, :], T.mi[:, :], T.pif[:, :], A.is_equal, -float(COLS), A.mult)
+    d1s = ts(T.d1s[:, :], T.mi[:, :], T.pm1[:, :], A.is_equal, T.kcol[:, :], A.mult, [pm1, kcol])
+    d2s = ts(T.d2s[:, :], T.mi[:, :], T.p15[:, :], A.is_equal, T.zc[:, :], A.mult, [p15, zc])
+
+    n_loc0 = n_loc1 = 0
+    if later:
+        rid, pnc = topo.addr(T.cores[r + 1], core)
+        after("g", [ca, tz])
+        g.remote_dma(T.ha[:, 0:16], T.ca[:, 128:144], T.sem["t"], T.sem["loc0"], pnc, rid, topo.mask(core, T.cores[r + 1]))
+        n_loc0 = len(topo.engines(core, T.cores[r + 1]))
+        after("g", [sm])
+        ids = []
+        for d in reversed(later):
+            rid, pnc = topo.addr(T.cores[d], core)
+            ids.append(DstId(rid=rid, pnc=pnc))
+        g.remote_dma_fused([RemoteDMATransfer(dst_ids=ids, dma_engine_mask=topo.mask(core, T.cores[later[0]]),
+                                              remote_sem=T.sem["m%d" % r], srcs=[T.sm[:, 33:65]],
+                                              dsts=[T["msg%d" % r][:, :] for d in later])], local_sem=T.sem["loc1"])
+        n_loc1 = len(topo.engines(core, T.cores[later[0]]))
+    wf = do("g", lambda e: e.iota(T.win[:, 0:COLS], [[0, COLS]], -2, 0, allow_small_or_imprecise_dtypes=True))
+
+    rst = act(T.rst[0:32, :], T.cb[0:32, :], F.Copy, bias=-2.0, scale=float(1 << 17), deps=[cb])
+    if r:
+        hac = act(T.ha[0:64, 16:48], T.ca[0:64, 0:32], F.Copy, deps=[ca])
+    psw = {}
+    for a in (2, 3, 0, 1):
+        lo = 16 if a else 0
+        psw[a] = mat(T["psw%d" % (a // 2)][:, 128 * (a % 2):128 * (a % 2) + 128], T["sel%d" % a][0:64, :], T.cp[0:64, lo:lo + 128],
+                     True, True, [sel[a], cp])
+        if a == 3:
+            v1 = mat(T.psv[:, 0:32], T.lvv[:, :], T.f2[:, :], True, False, [lvv, f2])
+            v2 = mat(T.psv[:, 0:32], T.sgv[:, :], T.s2[:, :], False, True, [sgv, s2])
+    psr = []
+    for a in range(4):
+        lo = 16 if a else 0
+        psr.append(mat(T.psr[:, 128 * a:128 * a + 128], T["sel%d" % a][0:32, :], T.rst[0:32, lo:lo + 128], True, True, [rst]))
+    mask = {}
+
+    def masks(h):
+        mask[h] = act(T.mask[:, 256 * h:256 * h + 256], T["psw%d" % h][:, 0:256], F.Square, bias=T.mb[:, :], scale=2048.0,
+                      deps=[psw[2 * h], psw[2 * h + 1], mb])
+    masks(1)
+    sgr = act(T.sgr[:, :], T.sg[:, :], F.Copy, scale=float(H))
+    ltr = act(T.ltr[:, :], T.lt[:, :], F.Copy, scale=-float(H))
+    masks(0)
+    pcol = act(T.pcol[:, :], T.paf[:, :], F.Copy, scale=float(COLS),
+               bias=float(COLS - H - 16 * r * H + 129 * (COLS - 1) - 2 * r))
+
+    mn = tt(T.mn[:, :], T.lw[:, 32:64], T.psv[:, 0:32], A.min, [v1, v2])
+    offv = ts(T.offv[:, :], T.mn[:, :], 1024.0, A.mult, -1017.0, A.add, [mn])
+
+    def gather(lo, hi, in1, deps):
+        return tt(T.mm[:, lo:hi], T.vw[:, :].indirect(T.offv[:, lo // 16:hi // 16]), in1, A.subtract, deps)
+    mm = [gather(256, 512, T.mask[:, 256:512], [l_val, offv, mask[1]] + vn)]
+    heads = [("m%d" % p, len(topo.engines(T.cores[p], core))) for p in range(r)]
+    p1 = [mat(T.ps1[:, 0:32], T.sgr[:, :], T.sm[:, 0:32], True, False, [sgr, sm]),
+          mat(T.ps1[:, 0:32], T.ltr[:, :], T.ff[:, 0:32], False, not r, [ltr, f0])]
+    p2 = [mat(T.ps2[:, 0:32], T.sgr[:, :], T.sm[:, 0:32], True, False),
+          mat(T.ps2[:, 0:32], T.ltr[:, :], T.ff[:, 0:32], False, False),
+          mat(T.ps2[:, 0:32], T.d1s[:, :], T.ff[:, 0:32], False, False, [d1s]),
+          mat(T.ps2[:, 0:32], T.d2s[:, :], T.ff[:, 1:33], False, False, [d2s, f1])]
+    if r:
+        hb = ts(T.hb[0:64, :], T.ha[0:64, :], 4.5, A.is_le, 16.0, A.mult, [hac, ("t", len(topo.engines(T.cores[r - 1], core)))])
+        hp = scan(T.hp[0:64, :], T.ha[0:64, :], T.hb[0:64, :], 0.0, A.add, A.min, [hb])
+        psh = mat(T.psh[:, 0:32], T.sel0[0:64, :], T.hp[0:64, 16:48], True, True, [hp])
+        maskh = act(T.maskh[:, :], T.psh[:, 0:32], F.Square, bias=T.mb[:, :], scale=2048.0, deps=[psh])
+        for p in range(r):
+            p1.append(mat(T.ps1[:, 0:32], T.sgr[:, :], T["msg%d" % p][:, :], False, p == r - 1, [heads[p]]))
+        for p in range(r):
+            p2.append(mat(T.ps2[:, 0:32], T.sgr[:, :], T["msg%d" % p][:, :], False, False))
+    mm.append(gather(32 if r else 0, 256, T.mask[:, 32 if r else 0:256], [mask[0]]))
+    if r:
+        mm.append(gather(0, 32, T.maskh[:, :], [maskh]))
+    hh = ts(T.hh[:, :], T.ps1[:, 0:32], 1.0 / COLS, A.mult, 129.0 - 17.0 / 32 - r, A.add, p1)
+    p2.append(mat(T.ps2[:, 0:32], T.idn[:, :], T.hh[:, :], False, False, [hh, idn]))
+    p2.append(mat(T.ps2[:, 0:32], T.idh[:, :], T.hh[:, :], False, True, [idh]))
+    vv = scan(T.vv[:, :], T.psr[:, :], T.mm[:, :], -2.0, A.min, A.max, psr + mm)
+    offs = ts(T.offs[:, :], T.ps2[:, 0:32], T.pcol[:, :], A.add, deps=p2 + [pcol])
+
+    sc = do("v", lambda e: e.tensor_copy(T.win[:, :].indirect(T.offs[:, :]), T.vv[:, :]), [offs, vv, wf])
+
+    after("g", [sc])
+    n_loc2 = 0
+    for k in range(1, N):
+        d = (r + k) % N
+        rid, pnc = topo.addr(T.cores[d], core)
+        g.remote_dma(T["from%d" % r][:, :, :], T.win[:, BLK * d:BLK * d + BLK], T.sem["h%d" % r], T.sem["loc2"],
+                     pnc, rid, topo.mask(core, T.cores[d]))
+        n_loc2 += len(topo.engines(core, T.cores[d]))
+    az = do("v", lambda e: e.memset(T.acc[:, :, :], -2.0))
+    m = [do("v", lambda e: e.tensor_copy(T.acc[:, b, 2 * r:2 * r + H], T.win[:, BLK * r + H * b:BLK * r + H * b + H]), [az, sc])
+         for b in range(4)]
+    for k in range(1, N):
+        p = (r - k) % N
+        part = T.acc[:, :, 2 * p:2 * p + H]
+        m = [tt(part, part, T["from%d" % p][:, :, :], A.max, m + [("h%d" % p, len(topo.engines(T.cores[p], core)))])]
+    ta = [do("v", lambda e: e.transpose(T.ta[:, b, :], T.acc[:, b, :]), m) for b in range(4)]
+    fin = [do("v", lambda e: e.tensor_copy(T.fin[:, 0, :, :], T.ta[:, :, 0:16]), ta),
+           act(T.fin[:, 1, :, :], T.ta[:, :, 16:32], F.Copy, deps=ta)]
+    for h, q in enumerate("ys"):
+        after(q, [fin[h]])
+        n = new()
+        queues[q].dma_start(T.y[h::2, :], T.fin[:, h, :, :]).then_inc(T.sem[n], 16)
+        after(q, [(n, 16)])
+
+    for n, c in (("loc0", n_loc0), ("loc1", n_loc1), ("loc2", n_loc2)):
+        if c:
+            g.wait_ge(T.sem[n], c)
+    waited = [d[0] for q in seen for d in seen[q]]
+    for n in used:
+        if n not in waited:
+            g.wait_ge(T.sem[n], 1)

@@ -2,8 +2,13 @@ from concourse.bass import DstId, RemoteDMATransfer
 from concourse.mybir import AluOpType as A, ActivationFunctionType as F
 
 H = 26
-BLK, COLS = 4 * H, 16 * H
-WINW = 17 * COLS
+BLK = 4 * H
+J = 352
+W = 448
+LOW = J + 8
+FILL = LOW + 512 - J + 8
+G0, Z = 16 * W, 16 * W + LOW
+S, UP = float(1 << 22), 64.0
 VWW = 16 + 512
 I32, F32, B16, U16 = "int32", "float32", "bfloat16", "uint16"
 
@@ -14,25 +19,24 @@ def sb(width, dtype):
 
 SCRATCH = {
     "lt0": sb(64, I32), "lw": sb(64, I32), "rlc": sb(144, I32), "vw": sb(VWW, I32),
-    "ff": sb(65, B16), "sm": sb(65, B16), "f2": sb(32, B16), "s2": sb(32, B16),
-    "mn": sb(32, F32), "offv": sb(32, U16), "offs": sb(32, U16), "hh": sb(32, B16),
-    "ca": sb(144, B16), "cb": sb(144, B16), "cp": sb(144, B16), "rst": sb(144, B16),
-    "ha": sb(48, B16), "hb": sb(48, B16), "hp": sb(48, B16),
-    "mask": sb(512, B16), "maskh": sb(32, B16), "mm": sb(512, F32), "vv": sb(512, F32), "win": sb(WINW, F32),
-    "msg0": sb(32, B16), "msg1": sb(32, B16), "msg2": sb(32, B16),
-    "from0": sb([4, H], F32), "from1": sb([4, H], F32), "from2": sb([4, H], F32), "from3": sb([4, H], F32),
-    "acc": sb([4, 32], F32), "ta": sb([4, 32], F32), "fin": sb([2, 4, 16], F32),
-    "mg": sb(128, B16), "mi": sb(128, B16), "sg": sb(128, B16), "lt": sb(128, B16), "idn": sb(128, B16), "idh": sb(128, B16),
+    "f0": sb(33, B16), "sm": sb(33, B16), "f2": sb(32, B16), "s2": sb(32, B16),
+    "mn": sb(32, F32), "offv": sb(32, U16), "offs": sb(34, U16), "lst": sb(32, U16), "tn0": sb(32, F32), "tn": sb(32, F32),
+    "ca": sb(144, B16), "cb": sb(144, B16), "cp": sb(144, B16),
+    "hm": sb(32, B16), "hx": sb(32, B16), "vh": sb(16, F32), "vx": sb(16, F32), "hp": sb(16, B16), "mh": sb(16, F32),
+    "mask": sb(512, B16), "mm": sb(512, F32), "vv": sb(528, F32), "win": sb(Z + 17 * W, F32),
+    "msg0": sb(16, B16), "msg1": sb(16, B16), "msg2": sb(16, B16),
+    "out1": sb(112, F32), "out2": sb(112, F32), "out3": sb(128, F32), "turned": sb([4, 32], F32),
+    "in1": sb(BLK, F32), "in2": sb(BLK, F32), "in3": sb([4, 32], F32),
+    "acc": sb(128, F32), "ta": sb([4, 32], F32), "fin": sb([2, 4, 16], F32),
+    "mg": sb(128, B16), "mgk": sb(128, B16), "sg": sb(128, B16), "lt": sb(128, B16), "sgk": sb(128, B16),
+    "dg": sb(128, B16), "dgn": sb(128, B16), "wrow": sb(128, B16), "half": sb(J, B16),
     "sel0": sb(128, B16), "sel1": sb(128, B16), "sel2": sb(128, B16), "sel3": sb(128, B16),
-    "sgv": sb(128, B16), "lvv": sb(128, B16), "sgr": sb(128, B16), "ltr": sb(128, B16),
-    "d1s": sb(128, B16), "d2s": sb(128, B16),
-    "pi": sb(1, I32), "pa": sb(1, I32), "kg": sb(1, I32), "pif": sb(1, F32), "paf": sb(1, F32), "kgf": sb(1, F32),
-    "kmod": sb(1, F32), "pm1": sb(1, F32), "p15": sb(1, F32), "zc": sb(1, F32),
-    "ccol": sb(1, F32), "mb": sb(1, F32), "pcol": sb(1, F32), "kcol": sb(1, F32),
+    "pin": sb(1, F32), "kgb": sb(1, B16), "pan": sb(1, F32), "kmod": sb(1, F32), "ccol": sb(1, F32),
+    "kcol": sb(1, F32), "acol": sb(1, F32), "p4": sb(1, B16), "qn": sb(1, F32), "hs": sb(1, F32), "hc": sb(1, F32),
 }
-for _b in ("ps1", "ps2", "psv", "psh", "psw0", "psw1", "psr"):
+for _b in ("ps2", "pst", "psv", "psh", "psa", "psb"):
     SCRATCH[_b] = ("psum", [128, 512], "float32")
-SEMAPHORES = ["s%d" % i for i in range(110)] + ["m0", "m1", "m2", "t", "h0", "h1", "h2", "h3", "loc0", "loc1", "loc2"]
+SEMAPHORES = ["s%d" % i for i in range(120)] + ["m0", "m1", "m2", "ta", "tv", "h1", "h2", "h3", "loc"]
 
 
 def rank_program(g, core, T, topo):
@@ -43,6 +47,7 @@ def rank_program(g, core, T, topo):
     queues = {"g": g, "v": g.vector, "s": g.scalar, "p": g.tensor, "y": g.sync}
     seen = {q: [] for q in queues}
     used = []
+    sent = [0]
 
     def after(q, deps):
         for d in deps:
@@ -66,6 +71,9 @@ def rank_program(g, core, T, topo):
             queues[q].dma_start(out, in_).then_inc(T.sem[n], 16)
         return (n, 16 * len(parts))
 
+    def fill(out, x):
+        return do("v", lambda e: e.memset(out, x))
+
     def ts(out, in0, s1, op0, s2=None, op1=None, deps=()):
         if op1 is None:
             return do("v", lambda e: e.tensor_scalar(out, in0, s1, None, op0), deps)
@@ -77,14 +85,31 @@ def rank_program(g, core, T, topo):
     def tt(out, in0, in1, op, deps=()):
         return do("v", lambda e: e.tensor_tensor(out, in0, in1, op), deps)
 
+    def turn(out, in_, deps=()):
+        return do("v", lambda e: e.transpose(out, in_), deps)
+
     def mat(out, lhs, rhs, start, stop, deps=()):
         return do("p", lambda e: e.matmul(out, lhs, rhs, start, stop), deps)
 
     def act(out, in_, func, bias=0.0, scale=1.0, deps=()):
         return do("s", lambda e: e.activation(out, in_, func, bias=bias, scale=scale), deps)
 
+    def iota(out, pattern, base, per_partition):
+        return do("g", lambda e: e.iota(out, pattern, base, per_partition, allow_small_or_imprecise_dtypes=True))
+
+    def send(d, out, in_, sem, deps):
+        after("g", deps)
+        rid, pnc = topo.addr(T.cores[d], core)
+        g.remote_dma(out, in_, T.sem[sem], T.sem["loc"], pnc, rid, topo.mask(core, T.cores[d]))
+        sent[0] += len(topo.engines(core, T.cores[d]))
+
+    def landed(sem, p):
+        return (sem, len(topo.engines(T.cores[p], core)))
+
     blk = [(a - r) % 4 for a in range(4)]
     later = [d for d in range(r + 1, N)]
+    dest = [(r + k) % N for k in range(N)]
+    c = J // 16
 
     parts = []
     for a in range(4):
@@ -94,151 +119,142 @@ def rank_program(g, core, T, topo):
     l_rlc = load(parts)
     l_lst = load([("y", T.lt0[:, 0:16], T.rl[0::2, :]), ("s", T.lt0[:, 16:32], T.rl[1::2, :]),
                   ("y", T.lt0[:, 32:48], T.dl[0::2, :]), ("s", T.lt0[:, 48:64], T.dl[1::2, :])])
+    l_val = load([("sy"[w > 3], T.vw[w::16, 16:528], T.val[:, :]) for w in range(16)])
 
-    pi = do("g", lambda e: e.iota(T.pi[:, :], [[0, 1]], 0, 1))
-    mg = do("g", lambda e: e.iota(T.mg[:, :], [[1, 8], [0, 16]], 0, 0, allow_small_or_imprecise_dtypes=True))
-    mi = do("g", lambda e: e.iota(T.mi[:, :], [[1, 128]], 0, 0, allow_small_or_imprecise_dtypes=True))
-    cc = [do("v", lambda e: e.memset(T.ccol[32 * i:32 * i + 32, :], 8.0 + i)) for i in range(2)]
-    fz = do("v", lambda e: e.memset(T.ff[:, 33:65], 0.0))
-    f1 = do("v", lambda e: e.memset(T.ff[:, 32:33], 1.0))
-    tz = do("v", lambda e: e.memset(T.ca[64:128, 128:144], 0.0)) if later else None
-    vn = [do("v", lambda e: e.memset(T.vw[:, 0:4], -2)), do("v", lambda e: e.memset(T.vw[:, 4:16], -1))]
-    pif = do("v", lambda e: e.tensor_copy(T.pif[:, :], T.pi[:, :]), [pi])
-    kg = ts(T.kg[:, :], T.pi[:, :], 4, A.arith_shift_right)
-    pa = ts(T.pa[:, :], T.pi[:, :], 15, A.bitwise_and)
-    kgf = do("v", lambda e: e.tensor_copy(T.kgf[:, :], T.kg[:, :]), [kg])
-    paf = do("v", lambda e: e.tensor_copy(T.paf[:, :], T.pa[:, :]), [pa])
-    sg = ts(T.sg[:, :], T.mg[:, :], T.kgf[:, :], A.is_equal, deps=[mg, kgf])
-    lt = do("g", lambda e: e.affine_select(T.lt[:, :], T.sg[:, :], [[-1, 128]], A.is_ge, 0.0, -1, 1), [sg])
-    km = [act(T.kmod[32 * i:32 * i + 32, :], T.pif[32 * i:32 * i + 32, :], F.Copy, bias=-32.0 * i, deps=[pif]) for i in range(2)]
-    l_val = load([("sy"[w > 5], T.vw[w::16, 16:528], T.val[:, :]) for w in range(16)])
-    zc = ts(T.zc[:, :], T.paf[:, :], 0.0, A.is_equal, -16.0 * COLS, A.mult, [paf])
-    sel = [ts(T["sel%d" % a][0:64, :], T.mg[0:64, :], 8.0 * blk[a], A.add, T.kmod[0:64, :], A.is_equal, km) for a in range(4)]
+    pin = iota(T.pin[:, :], [[0, 1]], 0, -1)
+    mg = iota(T.mg[:, :], [[1, 8], [0, 16]], 129, 0)
+    wrow = iota(T.wrow[:, :], [[0, 8], [2, 16]], 1, 0)
+    cc = [fill(T.ccol[32 * i:32 * i + 32, :], 8.0 + i) for i in range(2)]
+    half = fill(T.half[0:1, :], S / 2)
+    kgb = ts(T.kgb[:, :], T.pin[:, :], -1.0 / 16, A.mult, 129.0 - 7.5 / 16, A.add, [pin])
+    km = ts(T.kmod[0:64, :], T.ccol[0:64, :], 32.0, A.mult, T.pin[0:64, :], A.add, cc)
+    pan = ts(T.pan[:, :], T.kgb[:, :], -16.0, A.mult, T.pin[:, :], A.subtract, [kgb])
+    sg = ts(T.sg[:, :], T.mg[:, :], T.kgb[:, :], A.is_equal, deps=[mg])
+    lt = do("g", lambda e: e.affine_select(T.lt[:, :], T.sg[:, :], [[-1, 128]], A.is_ge, 0.0, 0, 1), [sg])
+    vn = do("g", lambda e: e.iota(T.vw[:, 0:16], [[1, 2], [0, 8]], -2, 0))
+    mgk = ts(T.mgk[0:64, :], T.mg[0:64, :], T.kmod[0:64, :], A.add, -256.0, A.add, [km])
+    kcol = ts(T.kcol[:, :], T.pan[:, :], 2065.0, A.add, -float(W), A.mult, [pan])
+    sel = [ts(T["sel%d" % a][0:64, :], T.mgk[0:64, :], 129.0 - 8 * blk[a], A.is_equal, -S, A.mult, [mgk]) for a in range(4)]
+    sgk = ts(T.sgk[:, :], T.sg[:, :], T.kcol[:, :], A.mult, deps=[kcol, sg])
+    fe = ts(T.f0[:, 32:33], T.pan[:, :], (15 if later else 0) - 2064.0, A.is_equal, -1.0, A.mult)
+    v0 = [fill(T.vv[:, 0:1], 0.0)] + ([] if later else [fill(T.vv[:, 513:528], 0.0)])
+    hz = iota(T.hm[:, :], [[0, 32]], 0, 0) if r else None
+    dg = do("g", lambda e: e.affine_select(T.dg[:, :], T.sgk[:, :], [[-1, 128]], A.is_equal, 0.0, 0, 1), [sgk])
+    hc = act(T.hc[0:64, :], T.ccol[0:64, :], F.Silu, bias=900.0, scale=-100.0, deps=cc)
+    hs = act(T.hs[0:64, :], T.ccol[0:64, :], F.Copy, bias=-3.5, scale=0.5)
+    banks = [(T.psa, 0, J), (T.psb, J, 512)]
+    for bank, lo, hi in banks + ([(T.psh, 0, 15)] if later else []):
+        mat(bank[:, 0:hi - lo], T.wrow[0:1, :], T.half[0:1, 0:hi - lo], True, False, [wrow, half])
 
-    mb = act(T.mb[:, :], T.paf[:, :], F.Copy, scale=-2048.0, deps=[paf])
-    kcol = act(T.kcol[:, :], T.paf[:, :], F.Copy, scale=-float(COLS))
-    pm1 = act(T.pm1[:, :], T.pif[:, :], F.Copy, bias=-1.0)
-    p15 = act(T.p15[:, :], T.pif[:, :], F.Copy, bias=15.0)
-    sgv = act(T.sgv[:, :], T.sg[:, :], F.Copy, scale=1.0 / 1024, deps=[sg])
-    lvv = act(T.lvv[:, :], T.lt[:, :], F.Copy, scale=-1.0 / 1024, deps=[lt])
-
-    ca = ts(T.ca[0:64, :], T.rlc[0:64, :], -4.0, A.mult, T.ccol[0:64, :], A.add, [l_rlc] + cc)
-    lw = do("v", lambda e: e.transpose(T.lw[:, :], T.lt0[:, :]), [l_lst])
+    ca = ts(T.ca[0:64, :], T.rlc[0:64, :], -4.0, A.mult, T.ccol[0:64, :], A.add, [l_rlc])
     cb = ts(T.cb[0:64, :], T.ca[0:64, :], 4.5, A.is_le, 16.0, A.mult, [ca])
-    f0 = ts(T.ff[:, 0:32], T.lw[:, 0:32], 0.0, A.is_equal, deps=[lw])
-    cp = scan(T.cp[0:64, :], T.ca[0:64, :], T.cb[0:64, :], 0.0, A.add, A.min, [cb])
-    sm = scan(T.sm[:, :], T.ff[:, :], T.ff[:, :], 0.0, A.add, A.max, [f0, f1, fz])
-    f2 = ts(T.f2[:, :], T.lw[:, 32:64], 2.0, A.is_equal)
-    s2 = scan(T.s2[:, :], T.f2[:, :], T.f2[:, :], 64.5, A.add, A.max, [f2])
-    idn = ts(T.idn[:, :], T.mi[:, :], T.pif[:, :], A.is_equal, deps=[mi])
-    idh = ts(T.idh[:, :], T.mi[:, :], T.pif[:, :], A.is_equal, -float(COLS), A.mult)
-    d1s = ts(T.d1s[:, :], T.mi[:, :], T.pm1[:, :], A.is_equal, T.kcol[:, :], A.mult, [pm1, kcol])
-    d2s = ts(T.d2s[:, :], T.mi[:, :], T.p15[:, :], A.is_equal, T.zc[:, :], A.mult, [p15, zc])
-
-    n_loc0 = n_loc1 = 0
+    cp = scan(T.cp[0:64, :], T.ca[0:64, :], T.cb[0:64, :], 16.0, A.add, A.min, [cb])
+    if r:
+        ha = act(T.hm[0:64, 0:16], T.ca[0:64, 0:16], F.Square, scale=T.hs[0:64, :], deps=[ca, hs, hz])
+        hb = act(T.hm[0:64, 16:32], T.cb[0:64, 0:16], F.Identity, bias=T.hc[0:64, :], deps=[cb, hc])
+        send(r - 1, T.hx[:, :], T.hm[:, :], "ta", [ha, hb])
+    lw = turn(T.lw[:, :], T.lt0[:, :], [l_lst])
+    f2 = ts(T.f2[:, :], T.lw[:, 32:64], 2.0, A.is_equal, -1.0 / 1024, A.mult, [lw])
+    f0 = ts(T.f0[:, 0:32], T.lw[:, 0:32], 0.0, A.is_equal, -1.0, A.mult)
+    s2 = scan(T.s2[:, :], T.f2[:, :], T.f2[:, :], 64.5 / 1024, A.max, A.subtract, [f2])
+    sm = scan(T.sm[:, :], T.f0[:, :], T.f0[:, :], 0.0, A.max, A.subtract, [f0, fe])
     if later:
-        rid, pnc = topo.addr(T.cores[r + 1], core)
-        after("g", [ca, tz])
-        g.remote_dma(T.ha[:, 0:16], T.ca[:, 128:144], T.sem["t"], T.sem["loc0"], pnc, rid, topo.mask(core, T.cores[r + 1]))
-        n_loc0 = len(topo.engines(core, T.cores[r + 1]))
         after("g", [sm])
         ids = []
-        for d in reversed(later):
+        for d in later:
             rid, pnc = topo.addr(T.cores[d], core)
             ids.append(DstId(rid=rid, pnc=pnc))
         g.remote_dma_fused([RemoteDMATransfer(dst_ids=ids, dma_engine_mask=topo.mask(core, T.cores[later[0]]),
-                                              remote_sem=T.sem["m%d" % r], srcs=[T.sm[:, 33:65]],
-                                              dsts=[T["msg%d" % r][:, :] for d in later])], local_sem=T.sem["loc1"])
-        n_loc1 = len(topo.engines(core, T.cores[later[0]]))
-    wf = do("g", lambda e: e.iota(T.win[:, 0:COLS], [[0, COLS]], -2, 0, allow_small_or_imprecise_dtypes=True))
+                                              remote_sem=T.sem["m%d" % r], srcs=[T.sm[:, 16:32]],
+                                              dsts=[T["msg%d" % r][:, :] for d in later])], local_sem=T.sem["loc"])
+        sent[0] += len(topo.engines(core, T.cores[later[0]]))
+    tn0 = [iota(T.tn0[:, 8 * i:8 * i + 8], [[64, 8]], LOW + 1 + 516 + 4 * dest[k] + (32 * r if k in (1, 2) else 0), 0)
+           for i, k in enumerate((1, 2, 3, 0))]
 
-    rst = act(T.rst[0:32, :], T.cb[0:32, :], F.Copy, bias=-2.0, scale=float(1 << 17), deps=[cb])
-    if r:
-        hac = act(T.ha[0:64, 16:48], T.ca[0:64, 0:32], F.Copy, deps=[ca])
-    psw = {}
-    for a in (2, 3, 0, 1):
-        lo = 16 if a else 0
-        psw[a] = mat(T["psw%d" % (a // 2)][:, 128 * (a % 2):128 * (a % 2) + 128], T["sel%d" % a][0:64, :], T.cp[0:64, lo:lo + 128],
-                     True, True, [sel[a], cp])
-        if a == 3:
-            v1 = mat(T.psv[:, 0:32], T.lvv[:, :], T.f2[:, :], True, False, [lvv, f2])
-            v2 = mat(T.psv[:, 0:32], T.sgv[:, :], T.s2[:, :], False, True, [sgv, s2])
-    psr = []
-    for a in range(4):
-        lo = 16 if a else 0
-        psr.append(mat(T.psr[:, 128 * a:128 * a + 128], T["sel%d" % a][0:32, :], T.rst[0:32, lo:lo + 128], True, True, [rst]))
-    mask = {}
-
-    def masks(h):
-        mask[h] = act(T.mask[:, 256 * h:256 * h + 256], T["psw%d" % h][:, 0:256], F.Square, bias=T.mb[:, :], scale=2048.0,
-                      deps=[psw[2 * h], psw[2 * h + 1], mb])
-    masks(1)
-    sgr = act(T.sgr[:, :], T.sg[:, :], F.Copy, scale=float(H))
-    ltr = act(T.ltr[:, :], T.lt[:, :], F.Copy, scale=-float(H))
-    masks(0)
-    pcol = act(T.pcol[:, :], T.paf[:, :], F.Copy, scale=float(COLS),
-               bias=float(COLS - H - 16 * r * H + 129 * (COLS - 1) - 2 * r))
+    psw = []
+    for bank, lo, hi in banks:
+        cuts = [lo] + [x for x in range(128, 512, 128) if lo < x < hi] + [hi]
+        for x0, x1 in zip(cuts, cuts[1:]):
+            a = x0 // 128
+            at = x0 - 128 * a + (16 if a else 0)
+            last = mat(bank[:, x0 - lo:x1 - lo], T["sel%d" % a][0:64, :], T.cp[0:64, at:at + x1 - x0], False, x1 == hi, [sel[a], cp])
+        psw.append(last)
+        if lo == 0:
+            v1 = mat(T.psv[:, 0:32], T.lt[:, :], T.f2[:, :], True, False, [lt, f2])
+            v2 = mat(T.psv[:, 0:32], T.sg[:, :], T.s2[:, :], False, True, [sg, s2])
+    acol = act(T.acol[:, :], T.kcol[:, :], F.Copy, bias=float(Z), deps=[kcol])
+    mask = [act(T.mask[:, lo:hi], bank[:, 0:hi - lo], F.Copy, bias=S / 2 + UP, scale=-1.0, deps=[psw[h]])
+            for h, (bank, lo, hi) in enumerate(banks)]
+    dgn = act(T.dgn[:, :], T.dg[:, :], F.Copy, scale=-1.0, deps=[dg])
+    wf = [act(T.win[:, G0:G0 + 512], T.mask[:, :], F.Copy, scale=0.0, deps=mask),
+          act(T.win[:, G0 + 512:G0 + FILL], T.mask[:, 0:FILL - 512], F.Copy, scale=0.0)]
 
     mn = tt(T.mn[:, :], T.lw[:, 32:64], T.psv[:, 0:32], A.min, [v1, v2])
-    offv = ts(T.offv[:, :], T.mn[:, :], 1024.0, A.mult, -1017.0, A.add, [mn])
-
-    def gather(lo, hi, in1, deps):
-        return tt(T.mm[:, lo:hi], T.vw[:, :].indirect(T.offv[:, lo // 16:hi // 16]), in1, A.subtract, deps)
-    mm = [gather(256, 512, T.mask[:, 256:512], [l_val, offv, mask[1]] + vn)]
-    heads = [("m%d" % p, len(topo.engines(T.cores[p], core))) for p in range(r)]
-    p1 = [mat(T.ps1[:, 0:32], T.sgr[:, :], T.sm[:, 0:32], True, False, [sgr, sm]),
-          mat(T.ps1[:, 0:32], T.ltr[:, :], T.ff[:, 0:32], False, not r, [ltr, f0])]
-    p2 = [mat(T.ps2[:, 0:32], T.sgr[:, :], T.sm[:, 0:32], True, False),
-          mat(T.ps2[:, 0:32], T.ltr[:, :], T.ff[:, 0:32], False, False),
-          mat(T.ps2[:, 0:32], T.d1s[:, :], T.ff[:, 0:32], False, False, [d1s]),
-          mat(T.ps2[:, 0:32], T.d2s[:, :], T.ff[:, 1:33], False, False, [d2s, f1])]
+    offv = ts(T.offv[:, :], T.mn[:, :], 1024.0, A.mult, -1016.0, A.add, [mn])
     if r:
-        hb = ts(T.hb[0:64, :], T.ha[0:64, :], 4.5, A.is_le, 16.0, A.mult, [hac, ("t", len(topo.engines(T.cores[r - 1], core)))])
-        hp = scan(T.hp[0:64, :], T.ha[0:64, :], T.hb[0:64, :], 0.0, A.add, A.min, [hb])
-        psh = mat(T.psh[:, 0:32], T.sel0[0:64, :], T.hp[0:64, 16:48], True, True, [hp])
-        maskh = act(T.maskh[:, :], T.psh[:, 0:32], F.Square, bias=T.mb[:, :], scale=2048.0, deps=[psh])
-        for p in range(r):
-            p1.append(mat(T.ps1[:, 0:32], T.sgr[:, :], T["msg%d" % p][:, :], False, p == r - 1, [heads[p]]))
-        for p in range(r):
-            p2.append(mat(T.ps2[:, 0:32], T.sgr[:, :], T["msg%d" % p][:, :], False, False))
-    mm.append(gather(32 if r else 0, 256, T.mask[:, 32 if r else 0:256], [mask[0]]))
-    if r:
-        mm.append(gather(0, 32, T.maskh[:, :], [maskh]))
-    hh = ts(T.hh[:, :], T.ps1[:, 0:32], 1.0 / COLS, A.mult, 129.0 - 17.0 / 32 - r, A.add, p1)
-    p2.append(mat(T.ps2[:, 0:32], T.idn[:, :], T.hh[:, :], False, False, [hh, idn]))
-    p2.append(mat(T.ps2[:, 0:32], T.idh[:, :], T.hh[:, :], False, True, [idh]))
-    vv = scan(T.vv[:, :], T.psr[:, :], T.mm[:, :], -2.0, A.min, A.max, psr + mm)
-    offs = ts(T.offs[:, :], T.ps2[:, 0:32], T.pcol[:, :], A.add, deps=p2 + [pcol])
+        vh = ts(T.vh[:, :], T.vw[:, :].indirect(T.offv[:, 0:1]), S / 2 + UP, A.add, deps=[l_val, offv, vn])
+        send(r - 1, T.vx[:, :], T.vh[:, :], "tv", [vh])
+    p2 = [mat(T.ps2[:, 0:33], T.sg[:, :], T.sm[:, :], True, False, [sm]),
+          mat(T.ps2[:, 0:33], T.lt[:, :], T.f0[:, :], False, False),
+          mat(T.ps2[:, 0:c], T.dg[:, :], T.f0[:, 0:c], False, False, [dg]),
+          mat(T.ps2[:, c:33], T.dgn[:, :], T.f0[:, c:33], False, True, [dgn]),
+          mat(T.ps2[:, 40:41], T.sg[:, :], T.sm[:, c - 1:c], True, True)]
 
-    sc = do("v", lambda e: e.tensor_copy(T.win[:, :].indirect(T.offs[:, :]), T.vv[:, :]), [offs, vv, wf])
+    def gather(lo, hi, deps):
+        return tt(T.mm[:, lo:hi], T.vw[:, :].indirect(T.offv[:, lo // 16:hi // 16]), T.mask[:, lo:hi], A.add, deps)
+    mm = gather(0, J, [l_val, offv, vn, mask[0]])
+    offa = ts(T.offs[:, 0:c], T.ps2[:, 0:c], T.ps2[:, 40:41], A.subtract, T.acol[:, :], A.add, p2 + [acol])
+    va = scan(T.vv[:, 1:J + 1], T.psa[:, 0:J], T.mm[:, 0:J], 0.0, A.max, A.min, [mm])
+    p4 = act(T.p4[:, :], T.pan[:, :], F.Copy, bias=516.0 + 129.0 - 0.375, scale=0.25)
+    qn = act(T.qn[:, :], T.p4[:, :], F.Identity, bias=T.pan[:, :], scale=12.0, deps=[p4])
+    tn = act(T.tn[:, :], T.tn0[:, :], F.Identity, bias=T.qn[:, :], deps=tn0 + [qn])
+    sa = do("s", lambda e: e.activation(T.win[:, 0:Z].indirect(T.offs[:, 0:c]), T.vv[:, 0:J], F.Silu), [offa, va] + v0 + wf)
+    mm = gather(J, 512, [mask[1]])
+    offb = ts(T.offs[:, c:33], T.ps2[:, c:33], T.ps2[:, 40:41], A.subtract, T.kcol[:, :], A.subtract)
+    if later:
+        hp = scan(T.hp[0:64, :], T.hx[0:64, 0:16], T.hx[0:64, 16:32], T.cp[0:64, 143:144], A.add, A.min, [landed("ta", r + 1)])
+        psh = mat(T.psh[:, 0:15], T.sel3[0:64, :], T.hp[0:64, 0:15], False, True, [hp])
+    vb = scan(T.vv[:, J + 1:513], T.psb[:, 0:512 - J], T.mm[:, J:512], T.vv[:, J:J + 1], A.max, A.min, [mm, va])
 
-    after("g", [sc])
-    n_loc2 = 0
-    for k in range(1, N):
-        d = (r + k) % N
-        rid, pnc = topo.addr(T.cores[d], core)
-        g.remote_dma(T["from%d" % r][:, :, :], T.win[:, BLK * d:BLK * d + BLK], T.sem["h%d" % r], T.sem["loc2"],
-                     pnc, rid, topo.mask(core, T.cores[d]))
-        n_loc2 += len(topo.engines(core, T.cores[d]))
-    az = do("v", lambda e: e.memset(T.acc[:, :, :], -2.0))
-    m = [do("v", lambda e: e.tensor_copy(T.acc[:, b, 2 * r:2 * r + H], T.win[:, BLK * r + H * b:BLK * r + H * b + H]), [az, sc])
-         for b in range(4)]
-    for k in range(1, N):
+    def scatter(lo, hi, deps):
+        return do("v", lambda e: e.tensor_copy(T.win[:, Z:Z + 17 * W].indirect(T.offs[:, lo // 16:hi // 16]), T.vv[:, lo:hi]), deps)
+    sb_ = scatter(J, 512 if later else 528, [offb, vb] + v0 + wf)
+    pt = [mat(T.pst[:, 0:1], T.sg[:, :], T.sm[:, c - 1:c], True, not r)]
+    for p in range(r):
+        pt.append(mat(T.pst[:, 0:1], T.sg[:, :], T["msg%d" % p][:, 15:16], False, p == r - 1, [landed("m%d" % p, p)]))
+    if later:
+        mh = tt(T.mh[:, 0:15], T.vx[:, 0:15], T.psh[:, 0:15], A.subtract, [psh, landed("tv", r + 1)])
+    lst = ts(T.lst[:, :], T.tn[:, :], T.pst[:, 0:1], A.subtract, FILL - 1.0, A.min, pt + [tn])
+    if later:
+        vc = scan(T.vv[:, 513:528], T.psh[:, 0:15], T.mh[:, 0:15], T.vv[:, 512:513], A.max, A.min, [mh])
+        sb_ = scatter(512, 528, [vc, sb_])
+
+    def pick(lo, hi):
+        return T.win[:, G0:G0 + FILL].indirect(T.lst[:, lo:hi])
+    ready = [sa, sb_, lst]
+    b1 = ts(T.out1[:, :], pick(0, 7), -UP, A.add, deps=ready)
+    b2 = act(T.out2[:, :], pick(8, 15), F.Copy, bias=-UP, deps=ready)
+    b3 = act(T.out3[:, :], pick(16, 24), F.Copy, bias=-UP)
+    own = ts(T.acc[:, :], pick(24, 32), -UP, A.add, -2.0, A.max)
+    b3 = [turn(T.turned[:, b, :], T.out3[:, b::4], [b3]) for b in range(4)]
+    send(dest[1], T.in1[:, :], T.out1[:, 0:BLK], "h1", [b1])
+    send(dest[2], T.in2[:, :], T.out2[:, 0:BLK], "h2", [b2])
+    send(dest[3], T.in3[:, :, :], T.turned[:, :, :], "h3", b3)
+    m = own
+    for k in (1, 2):
         p = (r - k) % N
-        part = T.acc[:, :, 2 * p:2 * p + H]
-        m = [tt(part, part, T["from%d" % p][:, :, :], A.max, m + [("h%d" % p, len(topo.engines(T.cores[p], core)))])]
-    ta = [do("v", lambda e: e.transpose(T.ta[:, b, :], T.acc[:, b, :]), m) for b in range(4)]
-    fin = [do("v", lambda e: e.tensor_copy(T.fin[:, 0, :, :], T.ta[:, :, 0:16]), ta),
-           act(T.fin[:, 1, :, :], T.ta[:, :, 16:32], F.Copy, deps=ta)]
+        part = T.acc[:, 8 * p:8 * p + BLK]
+        m = tt(part, part, T["in%d" % k][:, :], A.max, [m, landed("h%d" % k, p)])
+    ta = [turn(T.ta[:, b, :], T.acc[:, b::4], [m]) for b in range(4)]
     for h, q in enumerate("ys"):
-        after(q, [fin[h]])
+        fin = tt(T.fin[:, h, :, :], T.ta[:, :, 16 * h:16 * h + 16], T.in3[:, :, 16 * h:16 * h + 16], A.max,
+                 ta + [landed("h3", (r - 3) % N)])
+        after(q, [fin])
         n = new()
         queues[q].dma_start(T.y[h::2, :], T.fin[:, h, :, :]).then_inc(T.sem[n], 16)
         after(q, [(n, 16)])
 
-    for n, c in (("loc0", n_loc0), ("loc1", n_loc1), ("loc2", n_loc2)):
-        if c:
-            g.wait_ge(T.sem[n], c)
+    g.wait_ge(T.sem["loc"], sent[0])
     waited = [d[0] for q in seen for d in seen[q]]
     for n in used:
         if n not in waited:

@@ -3,13 +3,13 @@ from concourse.mybir import AluOpType as A, ActivationFunctionType as F
 
 H = 26
 BLK = 4 * H
-J = 352
-W = 448
+J = 368
+K = 512 - J + 16
+W = 512
 LOW = J + 8
 FILL = LOW + 512 - J + 8
 G0, Z = 16 * W, 16 * W + LOW
 S, UP = float(1 << 22), 64.0
-VWW = 16 + 512
 I32, F32, B16, U16 = "int32", "float32", "bfloat16", "uint16"
 
 
@@ -18,21 +18,22 @@ def sb(width, dtype):
 
 
 SCRATCH = {
-    "lt0": sb(64, I32), "lw": sb(64, I32), "rlc": sb(144, I32), "vw": sb(VWW, I32),
-    "f0": sb(33, B16), "sm": sb(33, B16), "f2": sb(32, B16), "s2": sb(32, B16),
-    "mn": sb(32, F32), "offv": sb(32, U16), "offs": sb(34, U16), "lst": sb(32, U16), "tn0": sb(32, F32), "tn": sb(32, F32),
+    "lt0": sb(64, I32), "lw": sb(64, I32), "rlc": sb(144, I32), "vw": sb(544, I32),
+    "f0": sb(33, B16), "sm": sb(33, B16), "f1": sb(32, B16), "f2": sb(32, B16), "s2": sb(32, B16),
+    "offv": sb(32, U16), "offa": sb(32, U16), "offb": sb(32, U16), "offc": sb(2, U16), "lst": sb(32, U16), "tn": sb(32, F32),
     "ca": sb(144, B16), "cb": sb(144, B16), "cp": sb(144, B16),
     "hm": sb(32, B16), "hx": sb(32, B16), "vh": sb(16, F32), "vx": sb(16, F32), "hp": sb(16, B16), "mh": sb(16, F32),
-    "mask": sb(512, B16), "mm": sb(512, F32), "vv": sb(528, F32), "win": sb(Z + 17 * W, F32),
+    "mask": sb(528, B16), "mm": sb(528, F32), "va": sb(J + 1, F32), "vb": sb(K + 16, F32), "win": sb(Z + 17 * W, F32),
     "msg0": sb(16, B16), "msg1": sb(16, B16), "msg2": sb(16, B16),
     "out1": sb(112, F32), "out2": sb(112, F32), "out3": sb(128, F32), "turned": sb([4, 32], F32),
     "in1": sb(BLK, F32), "in2": sb(BLK, F32), "in3": sb([4, 32], F32),
-    "acc": sb(128, F32), "ta": sb([4, 32], F32), "fin": sb([2, 4, 16], F32),
-    "mg": sb(128, B16), "mgk": sb(128, B16), "sg": sb(128, B16), "lt": sb(128, B16), "sgk": sb(128, B16),
-    "dg": sb(128, B16), "dgn": sb(128, B16), "wrow": sb(128, B16), "half": sb(J, B16),
+    "acc": sb(128, F32), "ta": ("psum", [128, 16, 32], F32), "fin": sb([2, 4, 16], F32),
+    "mi": sb(128, B16), "mg": sb(128, B16), "mgk": sb(128, B16), "sg": sb(128, B16), "lt": sb(128, B16),
+    "dg": sb(128, B16), "dgn": sb(128, B16), "step": sb(J, B16),
     "sel0": sb(128, B16), "sel1": sb(128, B16), "sel2": sb(128, B16), "sel3": sb(128, B16),
     "pin": sb(1, F32), "kgb": sb(1, B16), "pan": sb(1, F32), "kmod": sb(1, F32), "ccol": sb(1, F32),
-    "kcol": sb(1, F32), "acol": sb(1, F32), "p4": sb(1, B16), "qn": sb(1, F32), "hs": sb(1, F32), "hc": sb(1, F32),
+    "kcol": sb(1, F32), "acol": sb(1, F32), "p4": sb(1, B16), "qn": sb(1, F32), "u4": sb(1, B16),
+    "hs": sb(1, F32), "hc": sb(1, F32),
 }
 for _b in ("ps2", "pst", "psv", "psh", "psa", "psb"):
     SCRATCH[_b] = ("psum", [128, 512], "float32")
@@ -119,124 +120,121 @@ def rank_program(g, core, T, topo):
     l_rlc = load(parts)
     l_lst = load([("y", T.lt0[:, 0:16], T.rl[0::2, :]), ("s", T.lt0[:, 16:32], T.rl[1::2, :]),
                   ("y", T.lt0[:, 32:48], T.dl[0::2, :]), ("s", T.lt0[:, 48:64], T.dl[1::2, :])])
-    l_val = load([("sy"[w > 3], T.vw[w::16, 16:528], T.val[:, :]) for w in range(16)])
+    l_val = load([("sy"[w > 2], T.vw[w::16, 16:528], T.val[:, :]) for w in range(16)])
 
-    pin = iota(T.pin[:, :], [[0, 1]], 0, -1)
+    pin = iota(T.pin[:, :], [[0, 1]], 0, 1)
     mg = iota(T.mg[:, :], [[1, 8], [0, 16]], 129, 0)
-    wrow = iota(T.wrow[:, :], [[0, 8], [2, 16]], 1, 0)
-    cc = [fill(T.ccol[32 * i:32 * i + 32, :], 8.0 + i) for i in range(2)]
-    half = fill(T.half[0:1, :], S / 2)
-    kgb = ts(T.kgb[:, :], T.pin[:, :], -1.0 / 16, A.mult, 129.0 - 7.5 / 16, A.add, [pin])
-    km = ts(T.kmod[0:64, :], T.ccol[0:64, :], 32.0, A.mult, T.pin[0:64, :], A.add, cc)
-    pan = ts(T.pan[:, :], T.kgb[:, :], -16.0, A.mult, T.pin[:, :], A.subtract, [kgb])
-    sg = ts(T.sg[:, :], T.mg[:, :], T.kgb[:, :], A.is_equal, deps=[mg])
+    mi = iota(T.mi[:, :], [[1, 128]], 0, 0)
+    cc = [fill(T.ccol[32 * i:32 * i + 32, :], 2.0 + i / 4) for i in range(2)]
+    vn = [fill(T.vw[:, 0:16], -2), fill(T.vw[:, 528:544], -1)]
+    step = fill(T.step[:, :], -S / W)
+    kgb = ts(T.kgb[:, :], T.pin[:, :], 1.0 / 16, A.mult, 129.0 - 7.5 / 16, A.add, [pin])
+    km = ts(T.kmod[0:64, :], T.ccol[0:64, :], 128.0, A.mult, T.pin[0:64, :], A.subtract, cc)
+    v0 = [fill(T.va[:, 0:1], 0.0)] + ([] if later else [fill(T.vb[:, K + 1:K + 16], 0.0)])
+    pan = ts(T.pan[:, :], T.kgb[:, :], -16.0, A.mult, T.pin[:, :], A.add, [kgb])
+    mgk = ts(T.mgk[0:64, :], T.mg[0:64, :], T.kmod[0:64, :], A.add, -256.0, A.add, [mg, km])
+    sg = ts(T.sg[:, :], T.mg[:, :], T.kgb[:, :], A.is_equal)
     lt = do("g", lambda e: e.affine_select(T.lt[:, :], T.sg[:, :], [[-1, 128]], A.is_ge, 0.0, 0, 1), [sg])
-    vn = do("g", lambda e: e.iota(T.vw[:, 0:16], [[1, 2], [0, 8]], -2, 0))
-    mgk = ts(T.mgk[0:64, :], T.mg[0:64, :], T.kmod[0:64, :], A.add, -256.0, A.add, [km])
     kcol = ts(T.kcol[:, :], T.pan[:, :], 2065.0, A.add, -float(W), A.mult, [pan])
-    sel = [ts(T["sel%d" % a][0:64, :], T.mgk[0:64, :], 129.0 - 8 * blk[a], A.is_equal, -S, A.mult, [mgk]) for a in range(4)]
-    sgk = ts(T.sgk[:, :], T.sg[:, :], T.kcol[:, :], A.mult, deps=[kcol, sg])
     fe = ts(T.f0[:, 32:33], T.pan[:, :], (15 if later else 0) - 2064.0, A.is_equal, -1.0, A.mult)
-    v0 = [fill(T.vv[:, 0:1], 0.0)] + ([] if later else [fill(T.vv[:, 513:528], 0.0)])
+    sel = [ts(T["sel%d" % a][0:64, :], T.mgk[0:64, :], 129.0 - 8 * blk[a], A.is_equal, -16 * S, A.mult, [mgk]) for a in range(4)]
+    dg = ts(T.dg[:, :], T.mi[:, :], T.pin[:, :], A.is_equal, T.kcol[:, :], A.mult, [kcol, mi])
     hz = iota(T.hm[:, :], [[0, 32]], 0, 0) if r else None
-    dg = do("g", lambda e: e.affine_select(T.dg[:, :], T.sgk[:, :], [[-1, 128]], A.is_equal, 0.0, 0, 1), [sgk])
-    hc = act(T.hc[0:64, :], T.ccol[0:64, :], F.Silu, bias=900.0, scale=-100.0, deps=cc)
-    hs = act(T.hs[0:64, :], T.ccol[0:64, :], F.Copy, bias=-3.5, scale=0.5)
-    banks = [(T.psa, 0, J), (T.psb, J, 512)]
-    for bank, lo, hi in banks + ([(T.psh, 0, 15)] if later else []):
-        mat(bank[:, 0:hi - lo], T.wrow[0:1, :], T.half[0:1, 0:hi - lo], True, False, [wrow, half])
+    tn = [iota(T.tn[:, 16 * i:16 * i + 16], [[4 * (d1 - d0), 2], [64, 8]], LOW + 1 + 2064 + 48 + 4 * d0 + first, 1)
+          for i, (d0, d1, first) in enumerate(((dest[1], dest[2], 32 * r), (dest[3], r, 0)))]
+    hs = act(T.hs[0:64, :], T.ccol[0:64, :], F.Copy, bias=-14.0, scale=8.0, deps=cc)
+    hc = act(T.hc[0:64, :], T.ccol[0:64, :], F.Silu, bias=900.0, scale=-400.0)
+    banks = [(T.psa, 0, J, 0), (T.psb, J - 16, 512, J)]
+    for bank, lo, hi, _ in banks + ([(T.psh, 0, 15, 0)] if later else []):
+        mat(bank[:, 0:hi - lo], T.dg[:, :], T.step[:, 0:hi - lo], True, False, [dg, step])
 
-    ca = ts(T.ca[0:64, :], T.rlc[0:64, :], -4.0, A.mult, T.ccol[0:64, :], A.add, [l_rlc])
-    cb = ts(T.cb[0:64, :], T.ca[0:64, :], 4.5, A.is_le, 16.0, A.mult, [ca])
-    cp = scan(T.cp[0:64, :], T.ca[0:64, :], T.cb[0:64, :], 16.0, A.add, A.min, [cb])
+    ca = ts(T.ca[0:64, :], T.rlc[0:64, :], T.ccol[0:64, :], A.subtract, -0.25, A.mult, [l_rlc])
+    cb = ts(T.cb[0:64, :], T.rlc[0:64, :], T.ccol[0:64, :], A.subtract, -1.125, A.is_ge)
+    dgn = ts(T.dgn[:, :], T.dg[:, :], -1.0, A.mult, deps=[dg])
+    p4 = ts(T.p4[:, :], T.pan[:, :], 0.25, A.mult, 516.0 + 129.0 - 0.375, A.add)
+    cp = scan(T.cp[0:64, :], T.ca[0:64, :], T.cb[0:64, :], 1.0, A.add, A.min, [ca, cb])
     if r:
         ha = act(T.hm[0:64, 0:16], T.ca[0:64, 0:16], F.Square, scale=T.hs[0:64, :], deps=[ca, hs, hz])
         hb = act(T.hm[0:64, 16:32], T.cb[0:64, 0:16], F.Identity, bias=T.hc[0:64, :], deps=[cb, hc])
         send(r - 1, T.hx[:, :], T.hm[:, :], "ta", [ha, hb])
     lw = turn(T.lw[:, :], T.lt0[:, :], [l_lst])
-    f2 = ts(T.f2[:, :], T.lw[:, 32:64], 2.0, A.is_equal, -1.0 / 1024, A.mult, [lw])
+    acol = ts(T.acol[:, :], T.kcol[:, :], float(Z), A.add)
+    qn = ts(T.qn[:, :], T.p4[:, :], -4.0, A.mult, T.pan[:, :], A.add, [p4])
+    f2 = ts(T.f2[:, :], T.lw[:, 32:64], 2.0, A.is_equal, -1.0, A.mult, [lw])
     f0 = ts(T.f0[:, 0:32], T.lw[:, 0:32], 0.0, A.is_equal, -1.0, A.mult)
-    s2 = scan(T.s2[:, :], T.f2[:, :], T.f2[:, :], 64.5 / 1024, A.max, A.subtract, [f2])
+    f1 = ts(T.f1[:, :], T.lw[:, 32:64], 1.0, A.is_equal, -2.0, A.mult)
+    s2 = scan(T.s2[:, :], T.f2[:, :], T.f2[:, :], 1.0, A.max, A.subtract, [f2])
     sm = scan(T.sm[:, :], T.f0[:, :], T.f0[:, :], 0.0, A.max, A.subtract, [f0, fe])
-    if later:
-        after("g", [sm])
-        ids = []
-        for d in later:
-            rid, pnc = topo.addr(T.cores[d], core)
-            ids.append(DstId(rid=rid, pnc=pnc))
-        g.remote_dma_fused([RemoteDMATransfer(dst_ids=ids, dma_engine_mask=topo.mask(core, T.cores[later[0]]),
-                                              remote_sem=T.sem["m%d" % r], srcs=[T.sm[:, 16:32]],
-                                              dsts=[T["msg%d" % r][:, :] for d in later])], local_sem=T.sem["loc"])
-        sent[0] += len(topo.engines(core, T.cores[later[0]]))
-    tn0 = [iota(T.tn0[:, 8 * i:8 * i + 8], [[64, 8]], LOW + 1 + 516 + 4 * dest[k] + (32 * r if k in (1, 2) else 0), 0)
-           for i, k in enumerate((1, 2, 3, 0))]
+    u4 = ts(T.u4[:, :], T.qn[:, :], 3.0 - 2580, A.is_equal, 12.0, A.mult, [qn])
 
     psw = []
-    for bank, lo, hi in banks:
+    for bank, lo, hi, _ in banks:
         cuts = [lo] + [x for x in range(128, 512, 128) if lo < x < hi] + [hi]
         for x0, x1 in zip(cuts, cuts[1:]):
             a = x0 // 128
             at = x0 - 128 * a + (16 if a else 0)
             last = mat(bank[:, x0 - lo:x1 - lo], T["sel%d" % a][0:64, :], T.cp[0:64, at:at + x1 - x0], False, x1 == hi, [sel[a], cp])
         psw.append(last)
-        if lo == 0:
-            v1 = mat(T.psv[:, 0:32], T.lt[:, :], T.f2[:, :], True, False, [lt, f2])
-            v2 = mat(T.psv[:, 0:32], T.sg[:, :], T.s2[:, :], False, True, [sg, s2])
-    acol = act(T.acol[:, :], T.kcol[:, :], F.Copy, bias=float(Z), deps=[kcol])
-    mask = [act(T.mask[:, lo:hi], bank[:, 0:hi - lo], F.Copy, bias=S / 2 + UP, scale=-1.0, deps=[psw[h]])
-            for h, (bank, lo, hi) in enumerate(banks)]
-    dgn = act(T.dgn[:, :], T.dg[:, :], F.Copy, scale=-1.0, deps=[dg])
-    wf = [act(T.win[:, G0:G0 + 512], T.mask[:, :], F.Copy, scale=0.0, deps=mask),
-          act(T.win[:, G0 + 512:G0 + FILL], T.mask[:, 0:FILL - 512], F.Copy, scale=0.0)]
-
-    mn = tt(T.mn[:, :], T.lw[:, 32:64], T.psv[:, 0:32], A.min, [v1, v2])
-    offv = ts(T.offv[:, :], T.mn[:, :], 1024.0, A.mult, -1016.0, A.add, [mn])
-    if r:
-        vh = ts(T.vh[:, :], T.vw[:, :].indirect(T.offv[:, 0:1]), S / 2 + UP, A.add, deps=[l_val, offv, vn])
-        send(r - 1, T.vx[:, :], T.vh[:, :], "tv", [vh])
-    p2 = [mat(T.ps2[:, 0:33], T.sg[:, :], T.sm[:, :], True, False, [sm]),
-          mat(T.ps2[:, 0:33], T.lt[:, :], T.f0[:, :], False, False),
-          mat(T.ps2[:, 0:c], T.dg[:, :], T.f0[:, 0:c], False, False, [dg]),
-          mat(T.ps2[:, c:33], T.dgn[:, :], T.f0[:, c:33], False, True, [dgn]),
+    pv = [mat(T.psv[:, 0:32], T.lt[:, :], T.f2[:, :], True, False, [lt, f2]),
+          mat(T.psv[:, 0:32], T.dg[:, :], T.f2[:, :], False, False),
+          mat(T.psv[:, 0:32], T.dg[:, :], T.f1[:, :], False, False, [f1]),
+          mat(T.psv[:, 0:32], T.sg[:, :], T.s2[:, :], False, True, [sg, s2])]
+    mask = [act(T.mask[:, at:at + hi - lo], bank[:, 0:hi - lo], F.Copy, bias=S + UP, scale=-1.0, deps=[psw[h]])
+            for h, (bank, lo, hi, at) in enumerate(banks)]
+    wf = act(T.win[:, G0:G0 + FILL], T.mask[:, 0:FILL], F.Copy, scale=0.0, deps=mask)
+    p2 = [mat(T.ps2[:, 0:33], T.lt[:, :], T.f0[:, :], True, False, [f0, fe]),
+          mat(T.ps2[:, 0:c], T.dg[:, :], T.f0[:, 0:c], False, False),
+          mat(T.ps2[:, c:33], T.dgn[:, :], T.f0[:, c:33], False, False, [dgn]),
+          mat(T.ps2[:, 0:33], T.sg[:, :], T.sm[:, :], False, True, [sm]),
           mat(T.ps2[:, 40:41], T.sg[:, :], T.sm[:, c - 1:c], True, True)]
 
-    def gather(lo, hi, deps):
-        return tt(T.mm[:, lo:hi], T.vw[:, :].indirect(T.offv[:, lo // 16:hi // 16]), T.mask[:, lo:hi], A.add, deps)
-    mm = gather(0, J, [l_val, offv, vn, mask[0]])
-    offa = ts(T.offs[:, 0:c], T.ps2[:, 0:c], T.ps2[:, 40:41], A.subtract, T.acol[:, :], A.add, p2 + [acol])
-    va = scan(T.vv[:, 1:J + 1], T.psa[:, 0:J], T.mm[:, 0:J], 0.0, A.max, A.min, [mm])
-    p4 = act(T.p4[:, :], T.pan[:, :], F.Copy, bias=516.0 + 129.0 - 0.375, scale=0.25)
-    qn = act(T.qn[:, :], T.p4[:, :], F.Identity, bias=T.pan[:, :], scale=12.0, deps=[p4])
-    tn = act(T.tn[:, :], T.tn0[:, :], F.Identity, bias=T.qn[:, :], deps=tn0 + [qn])
-    sa = do("s", lambda e: e.activation(T.win[:, 0:Z].indirect(T.offs[:, 0:c]), T.vv[:, 0:J], F.Silu), [offa, va] + v0 + wf)
-    mm = gather(J, 512, [mask[1]])
-    offb = ts(T.offs[:, c:33], T.ps2[:, c:33], T.ps2[:, 40:41], A.subtract, T.kcol[:, :], A.subtract)
+    offv = ts(T.offv[:, :], T.psv[:, 0:32], T.kcol[:, :], A.add, 528.0, A.min, pv)
+    offa = ts(T.offa[:, 0:c], T.ps2[:, 0:c], T.ps2[:, 40:41], A.subtract, T.acol[:, :], A.add, p2 + [acol])
+    ends = [(T.offb, c, 32), (T.offc, 32, 33)] if later else [(T.offb, c, 33)]
+    offb = [ts(o[:, 0:hi - lo], T.ps2[:, lo:hi], T.ps2[:, 40:41], A.subtract, T.kcol[:, :], A.subtract) for o, lo, hi in ends]
+    if r:
+        vh = ts(T.vh[:, :], T.vw[:, :].indirect(T.offv[:, 0:1]), S + UP, A.add, deps=[l_val, offv] + vn)
+        send(r - 1, T.vx[:, :], T.vh[:, :], "tv", [vh])
+    if later:
+        after("g", [sm, l_val])
+        ids = [DstId(rid=rid, pnc=pnc) for rid, pnc in (topo.addr(T.cores[d], core) for d in later)]
+        g.remote_dma_fused([RemoteDMATransfer(dst_ids=ids, dma_engine_mask=topo.mask(core, T.cores[later[0]]),
+                                              remote_sem=T.sem["m%d" % r], srcs=[T.sm[:, 16:32]],
+                                              dsts=[T["msg%d" % r][:, :] for d in later])], local_sem=T.sem["loc"])
+        sent[0] += len(topo.engines(core, T.cores[later[0]]))
+    mm = [tt(T.mm[:, at:at + hi - lo], T.vw[:, :].indirect(T.offv[:, lo // 16:hi // 16]), T.mask[:, at:at + hi - lo], A.add,
+             [l_val, offv, mask[h]] + vn) for h, (bank, lo, hi, at) in enumerate(banks)]
+    va = scan(T.va[:, 1:J + 1], T.psa[:, 0:J], T.mm[:, 0:J], 0.0, A.max, A.min, [mm[0]])
+    sa = do("s", lambda e: e.activation(T.win[:, 0:Z].indirect(T.offa[:, 0:c]), T.va[:, 0:J], F.Silu), [offa, va, wf] + v0)
+    vb = scan(T.vb[:, 1:K + 1], T.psb[:, 0:K], T.mm[:, J:J + K], 0.0, A.max, A.min, [mm[1]])
     if later:
         hp = scan(T.hp[0:64, :], T.hx[0:64, 0:16], T.hx[0:64, 16:32], T.cp[0:64, 143:144], A.add, A.min, [landed("ta", r + 1)])
         psh = mat(T.psh[:, 0:15], T.sel3[0:64, :], T.hp[0:64, 0:15], False, True, [hp])
-    vb = scan(T.vv[:, J + 1:513], T.psb[:, 0:512 - J], T.mm[:, J:512], T.vv[:, J:J + 1], A.max, A.min, [mm, va])
-
-    def scatter(lo, hi, deps):
-        return do("v", lambda e: e.tensor_copy(T.win[:, Z:Z + 17 * W].indirect(T.offs[:, lo // 16:hi // 16]), T.vv[:, lo:hi]), deps)
-    sb_ = scatter(J, 512 if later else 528, [offb, vb] + v0 + wf)
-    pt = [mat(T.pst[:, 0:1], T.sg[:, :], T.sm[:, c - 1:c], True, not r)]
+    pt = [mat(T.pst[:, 0:1], T.sg[:, :], T.sm[:, c - 1:c], True, False),
+          mat(T.pst[:, 0:1], T.sg[:, :], T.kgb[:, :], False, False),
+          mat(T.pst[:, 0:1], T.lt[:, :], T.u4[:, :], False, not r, [u4])]
     for p in range(r):
         pt.append(mat(T.pst[:, 0:1], T.sg[:, :], T["msg%d" % p][:, 15:16], False, p == r - 1, [landed("m%d" % p, p)]))
+
+    def scatter(offsets, lo, hi, deps=(), at=16):
+        return do("v", lambda e: e.tensor_copy(T.win[:, Z:Z + 17 * W].indirect(offsets[:, lo:hi]),
+                                               T.vb[:, at + 16 * lo:at + 16 * hi]), deps)
+    sv = [scatter(T.offb, 0, (32 if later else 33) - c, offb + [vb, wf] + v0)]
     if later:
         mh = tt(T.mh[:, 0:15], T.vx[:, 0:15], T.psh[:, 0:15], A.subtract, [psh, landed("tv", r + 1)])
-    lst = ts(T.lst[:, :], T.tn[:, :], T.pst[:, 0:1], A.subtract, FILL - 1.0, A.min, pt + [tn])
+    lst = ts(T.lst[:, :], T.tn[:, :], T.pst[:, 0:1], A.subtract, FILL - 1.0, A.min, pt + tn)
     if later:
-        vc = scan(T.vv[:, 513:528], T.psh[:, 0:15], T.mh[:, 0:15], T.vv[:, 512:513], A.max, A.min, [mh])
-        sb_ = scatter(512, 528, [vc, sb_])
+        vc = scan(T.vb[:, K + 1:K + 16], T.psh[:, 0:15], T.mh[:, 0:15], T.vb[:, K:K + 1], A.max, A.min, [mh])
+        sv.append(scatter(T.offc, 0, 1, [vc] + sv, K))
 
     def pick(lo, hi):
         return T.win[:, G0:G0 + FILL].indirect(T.lst[:, lo:hi])
-    ready = [sa, sb_, lst]
+    ready = [sa, lst] + sv
     b1 = ts(T.out1[:, :], pick(0, 7), -UP, A.add, deps=ready)
-    b2 = act(T.out2[:, :], pick(8, 15), F.Copy, bias=-UP, deps=ready)
-    b3 = act(T.out3[:, :], pick(16, 24), F.Copy, bias=-UP)
-    own = ts(T.acc[:, :], pick(24, 32), -UP, A.add, -2.0, A.max)
+    b3 = act(T.out3[:, :], pick(16, 24), F.Copy, bias=-UP, deps=ready)
+    b2 = ts(T.out2[:, :], pick(8, 15), -UP, A.add)
     b3 = [turn(T.turned[:, b, :], T.out3[:, b::4], [b3]) for b in range(4)]
+    own = ts(T.acc[:, :], pick(24, 32), -UP, A.add, -2.0, A.max)
     send(dest[1], T.in1[:, :], T.out1[:, 0:BLK], "h1", [b1])
     send(dest[2], T.in2[:, :], T.out2[:, 0:BLK], "h2", [b2])
     send(dest[3], T.in3[:, :, :], T.turned[:, :, :], "h3", b3)
@@ -247,7 +245,7 @@ def rank_program(g, core, T, topo):
         m = tt(part, part, T["in%d" % k][:, :], A.max, [m, landed("h%d" % k, p)])
     ta = [turn(T.ta[:, b, :], T.acc[:, b::4], [m]) for b in range(4)]
     for h, q in enumerate("ys"):
-        fin = tt(T.fin[:, h, :, :], T.ta[:, :, 16 * h:16 * h + 16], T.in3[:, :, 16 * h:16 * h + 16], A.max,
+        fin = tt(T.fin[:, h, :, :], T.ta[:, 0:4, 16 * h:16 * h + 16], T.in3[:, :, 16 * h:16 * h + 16], A.max,
                  ta + [landed("h3", (r - 3) % N)])
         after(q, [fin])
         n = new()

@@ -3,7 +3,7 @@ from concourse.mybir import AluOpType as A, ActivationFunctionType as F
 
 H = 26
 BLK = 4 * H
-J = 368
+J = 320
 K = 512 - J + 16
 W = 512
 LOW = J + 8
@@ -31,7 +31,7 @@ SCRATCH = {
     "mi": sb(128, B16), "mg": sb(128, B16), "mgk": sb(128, B16), "sg": sb(128, B16), "lt": sb(128, B16),
     "dg": sb(128, B16), "dgn": sb(128, B16), "step": sb(J, B16),
     "sel0": sb(128, B16), "sel1": sb(128, B16), "sel2": sb(128, B16), "sel3": sb(128, B16),
-    "pin": sb(1, F32), "kgb": sb(1, B16), "pan": sb(1, F32), "kmod": sb(1, F32), "ccol": sb(1, F32),
+    "pin": sb(1, F32), "pw": sb(1, F32), "kgb": sb(1, B16), "pan": sb(1, F32), "kmod": sb(1, F32), "ccol": sb(1, F32),
     "kcol": sb(1, F32), "acol": sb(1, F32), "p4": sb(1, B16), "qn": sb(1, F32), "u4": sb(1, B16),
     "hs": sb(1, F32), "hc": sb(1, F32),
 }
@@ -107,106 +107,131 @@ def rank_program(g, core, T, topo):
     def landed(sem, p):
         return (sem, len(topo.engines(T.cores[p], core)))
 
+    def counts(to, deps):
+        after("g", deps)
+        ids = [DstId(rid=rid, pnc=pnc) for rid, pnc in (topo.addr(T.cores[d], core) for d in to)]
+        g.remote_dma_fused([RemoteDMATransfer(dst_ids=ids, dma_engine_mask=topo.mask(core, T.cores[to[0]]),
+                                              remote_sem=T.sem["m%d" % r], srcs=[T.sm[:, 16:32]],
+                                              dsts=[T["msg%d" % r][:, :] for d in to])], local_sem=T.sem["loc"])
+        sent[0] += len(topo.engines(core, T.cores[to[0]]))
+
     blk = [(a - r) % 4 for a in range(4)]
     later = [d for d in range(r + 1, N)]
     dest = [(r + k) % N for k in range(N)]
     c = J // 16
 
+    def lists(x, at):
+        return load([(q, T.lt0[:, at + 16 * h:at + 16 * h + 16], x[h::2, :]) for h, q in enumerate("ys")])
     parts = []
     for a in range(4):
         for q, row in (("y", 8 * blk[a]), ("s", 32 + 8 * blk[a])):
             lo = max(0, 128 * a - 16)
             parts.append((q, T.rlc[row:row + 8, :], T.rl[:, lo:lo + 144]))
     l_rlc = load(parts)
-    l_lst = load([("y", T.lt0[:, 0:16], T.rl[0::2, :]), ("s", T.lt0[:, 16:32], T.rl[1::2, :]),
-                  ("y", T.lt0[:, 32:48], T.dl[0::2, :]), ("s", T.lt0[:, 48:64], T.dl[1::2, :])])
-    l_val = load([("sy"[w > 2], T.vw[w::16, 16:528], T.val[:, :]) for w in range(16)])
+    l_lst = [lists(T.rl, 0), lists(T.dl, 32)]
+    l_val = load([("sy"[w > 5], T.vw[w::16, 16:528], T.val[:, :]) for w in range(16)])
 
     pin = iota(T.pin[:, :], [[0, 1]], 0, 1)
     mg = iota(T.mg[:, :], [[1, 8], [0, 16]], 129, 0)
     mi = iota(T.mi[:, :], [[1, 128]], 0, 0)
+    tn = [iota(T.tn[:, 16 * i:16 * i + 16], [[4 * (d1 - d0), 2], [64, 8]], LOW + 1 + 2064 + 48 + 4 * d0 + first, 1)
+          for i, (d0, d1, first) in enumerate(((dest[1], dest[2], 32 * r), (dest[3], r, 0)))]
     cc = [fill(T.ccol[32 * i:32 * i + 32, :], 2.0 + i / 4) for i in range(2)]
     vn = [fill(T.vw[:, 0:16], -2), fill(T.vw[:, 528:544], -1)]
+    v0 = [fill(T.va[:, 0:1], 0.0)] + ([] if later else [fill(T.vb[:, K + 1:K + 16], 0.0)])
     step = fill(T.step[:, :], -S / W)
     kgb = ts(T.kgb[:, :], T.pin[:, :], 1.0 / 16, A.mult, 129.0 - 7.5 / 16, A.add, [pin])
+    pw = ts(T.pw[:, :], T.pin[:, :], 2065.0, A.add, -float(W), A.mult)
     km = ts(T.kmod[0:64, :], T.ccol[0:64, :], 128.0, A.mult, T.pin[0:64, :], A.subtract, cc)
-    v0 = [fill(T.va[:, 0:1], 0.0)] + ([] if later else [fill(T.vb[:, K + 1:K + 16], 0.0)])
-    pan = ts(T.pan[:, :], T.kgb[:, :], -16.0, A.mult, T.pin[:, :], A.add, [kgb])
+    if r:
+        hz = fill(T.hm[64:128, :], 0.0)
+        hs = ts(T.hs[0:64, :], T.ccol[0:64, :], 3.125, A.mult, -7.0, A.add)
+        hc = ts(T.hc[0:64, :], T.ccol[0:64, :], 409.0, A.mult, -918.0, A.add)
+    kcol = ts(T.kcol[:, :], T.kgb[:, :], 16.0 * W, A.mult, T.pw[:, :], A.add, [kgb, pw])
     mgk = ts(T.mgk[0:64, :], T.mg[0:64, :], T.kmod[0:64, :], A.add, -256.0, A.add, [mg, km])
     sg = ts(T.sg[:, :], T.mg[:, :], T.kgb[:, :], A.is_equal)
     lt = do("g", lambda e: e.affine_select(T.lt[:, :], T.sg[:, :], [[-1, 128]], A.is_ge, 0.0, 0, 1), [sg])
-    kcol = ts(T.kcol[:, :], T.pan[:, :], 2065.0, A.add, -float(W), A.mult, [pan])
-    fe = ts(T.f0[:, 32:33], T.pan[:, :], (15 if later else 0) - 2064.0, A.is_equal, -1.0, A.mult)
-    sel = [ts(T["sel%d" % a][0:64, :], T.mgk[0:64, :], 129.0 - 8 * blk[a], A.is_equal, -16 * S, A.mult, [mgk]) for a in range(4)]
+    pan = ts(T.pan[:, :], T.kgb[:, :], -16.0, A.mult, T.pin[:, :], A.add)
     dg = ts(T.dg[:, :], T.mi[:, :], T.pin[:, :], A.is_equal, T.kcol[:, :], A.mult, [kcol, mi])
-    hz = iota(T.hm[:, :], [[0, 32]], 0, 0) if r else None
-    tn = [iota(T.tn[:, 16 * i:16 * i + 16], [[4 * (d1 - d0), 2], [64, 8]], LOW + 1 + 2064 + 48 + 4 * d0 + first, 1)
-          for i, (d0, d1, first) in enumerate(((dest[1], dest[2], 32 * r), (dest[3], r, 0)))]
-    hs = act(T.hs[0:64, :], T.ccol[0:64, :], F.Copy, bias=-14.0, scale=8.0, deps=cc)
-    hc = act(T.hc[0:64, :], T.ccol[0:64, :], F.Silu, bias=900.0, scale=-400.0)
-    banks = [(T.psa, 0, J, 0), (T.psb, J - 16, 512, J)]
-    for bank, lo, hi, _ in banks + ([(T.psh, 0, 15, 0)] if later else []):
-        mat(bank[:, 0:hi - lo], T.dg[:, :], T.step[:, 0:hi - lo], True, False, [dg, step])
+    acol = act(T.acol[:, :], T.kcol[:, :], F.Silu, bias=float(Z), deps=[kcol])
+    for bank, n in [(T.psb, K + 32), (T.psa, J)]:
+        mat(bank[:, 0:n], T.dg[:, :], T.step[:, 0:n], True, False, [dg, step])
 
-    ca = ts(T.ca[0:64, :], T.rlc[0:64, :], T.ccol[0:64, :], A.subtract, -0.25, A.mult, [l_rlc])
-    cb = ts(T.cb[0:64, :], T.rlc[0:64, :], T.ccol[0:64, :], A.subtract, -1.125, A.is_ge)
-    dgn = ts(T.dgn[:, :], T.dg[:, :], -1.0, A.mult, deps=[dg])
-    p4 = ts(T.p4[:, :], T.pan[:, :], 0.25, A.mult, 516.0 + 129.0 - 0.375, A.add)
-    cp = scan(T.cp[0:64, :], T.ca[0:64, :], T.cb[0:64, :], 1.0, A.add, A.min, [ca, cb])
+    def select(a):
+        return ts(T["sel%d" % a][0:64, :], T.mgk[0:64, :], 129.0 - 8 * blk[a], A.is_equal, -16 * S, A.mult, [mgk])
+    sel = {a: select(a) for a in (2, 3)}
+
     if r:
-        ha = act(T.hm[0:64, 0:16], T.ca[0:64, 0:16], F.Square, scale=T.hs[0:64, :], deps=[ca, hs, hz])
-        hb = act(T.hm[0:64, 16:32], T.cb[0:64, 0:16], F.Identity, bias=T.hc[0:64, :], deps=[cb, hc])
-        send(r - 1, T.hx[:, :], T.hm[:, :], "ta", [ha, hb])
-    lw = turn(T.lw[:, :], T.lt0[:, :], [l_lst])
-    acol = ts(T.acol[:, :], T.kcol[:, :], float(Z), A.add)
-    qn = ts(T.qn[:, :], T.p4[:, :], -4.0, A.mult, T.pan[:, :], A.add, [p4])
-    f2 = ts(T.f2[:, :], T.lw[:, 32:64], 2.0, A.is_equal, -1.0, A.mult, [lw])
-    f0 = ts(T.f0[:, 0:32], T.lw[:, 0:32], 0.0, A.is_equal, -1.0, A.mult)
-    f1 = ts(T.f1[:, :], T.lw[:, 32:64], 1.0, A.is_equal, -2.0, A.mult)
-    s2 = scan(T.s2[:, :], T.f2[:, :], T.f2[:, :], 1.0, A.max, A.subtract, [f2])
-    sm = scan(T.sm[:, :], T.f0[:, :], T.f0[:, :], 0.0, A.max, A.subtract, [f0, fe])
-    u4 = ts(T.u4[:, :], T.qn[:, :], 3.0 - 2580, A.is_equal, 12.0, A.mult, [qn])
+        ha = ts(T.hm[0:64, 0:16], T.rlc[0:64, 0:16], T.hs[0:64, :], A.mult, -1.0, A.max, [hs, l_rlc])
+        hb = ts(T.hm[0:64, 16:32], T.rlc[0:64, 0:16], T.hc[0:64, :], A.subtract, -1.125, A.is_ge, [hc])
+        send(r - 1, T.hx[:, :], T.hm[:, :], "ta", [hz, ha, hb])
+    calls = {
+        "ca": lambda: ts(T.ca[0:64, :], T.rlc[0:64, :], T.ccol[0:64, :], A.subtract, -0.25, A.mult, [l_rlc]),
+        "cb": lambda: ts(T.cb[0:64, :], T.rlc[0:64, :], T.ccol[0:64, :], A.subtract, -1.125, A.is_ge, [l_rlc]),
+        "cp": lambda: scan(T.cp[0:64, :], T.ca[0:64, :], T.cb[0:64, :], 1.0, A.add, A.min, [made["ca"], made["cb"]]),
+        "dgn": lambda: ts(T.dgn[:, :], T.dg[:, :], -1.0, A.mult, deps=[dg]),
+        "lw0": lambda: turn(T.lw[:, 0:32], T.lt0[:, 0:32], [l_lst[0]]),
+        "lw2": lambda: turn(T.lw[:, 32:64], T.lt0[:, 32:64], [l_lst[1]]),
+        "f0": lambda: ts(T.f0[:, 0:32], T.lw[:, 0:32], 0.0, A.is_equal, -1.0, A.mult, [made["lw0"]]),
+        "f1": lambda: ts(T.f1[:, :], T.lw[:, 32:64], 1.0, A.is_equal, -2.0, A.mult, [made["lw2"]]),
+        "f2": lambda: ts(T.f2[:, :], T.lw[:, 32:64], 2.0, A.is_equal, -1.0, A.mult, [made["lw2"]]),
+        "sm": lambda: scan(T.sm[:, :], T.f0[:, :], T.f0[:, :], 0.0, A.max, A.subtract, [made["f0"], made["fe"]]),
+        "fe": lambda: ts(T.f0[:, 32:33], T.pan[:, :], (15 if later else 0) - 2064.0, A.is_equal, -1.0, A.mult, [pan]),
+        "sel0": lambda: select(0),
+        "sel1": lambda: select(1),
+        "s2": lambda: scan(T.s2[:, :], T.f2[:, :], T.f2[:, :], 1.0, A.max, A.subtract, [made["f2"]]),
+    }
+    made = {}
+    for name in "ca cb lw0 sel0 fe lw2 cp f0 sel1 f2 f1 sm dgn s2".split():
+        made[name] = calls[name]()
+    cp, dgn, fe, f0, f1, f2, sm, s2 = (made[name] for name in "cp dgn fe f0 f1 f2 sm s2".split())
+    sel.update({0: made["sel0"], 1: made["sel1"]})
+    if later:
+        counts(later, [sm, s2])
 
-    psw = []
-    for bank, lo, hi, _ in banks:
-        cuts = [lo] + [x for x in range(128, 512, 128) if lo < x < hi] + [hi]
-        for x0, x1 in zip(cuts, cuts[1:]):
-            a = x0 // 128
-            at = x0 - 128 * a + (16 if a else 0)
-            last = mat(bank[:, x0 - lo:x1 - lo], T["sel%d" % a][0:64, :], T.cp[0:64, at:at + x1 - x0], False, x1 == hi, [sel[a], cp])
-        psw.append(last)
+    def plane(bank, lo, x0, x1, stop):
+        a = x0 // 128
+        at = x0 - 128 * a + (16 if a else 0)
+        return mat(bank[:, x0 - lo:x1 - lo], T["sel%d" % a][0:64, :], T.cp[0:64, at:at + x1 - x0], False, stop, [sel[a], cp])
+
+    def masks(bank, lo, end, last):
+        return act(T.mask[:, lo:end], bank[:, 0:end - lo], F.Copy, bias=S + UP, scale=-1.0, deps=[last])
+    plane(T.psb, J - 32, J - 32, 384, False)
+    mask = [masks(T.psb, J - 32, 528, plane(T.psb, J - 32, 384, 512, True))]
+    plane(T.psa, 0, 0, 128, False)
     pv = [mat(T.psv[:, 0:32], T.lt[:, :], T.f2[:, :], True, False, [lt, f2]),
           mat(T.psv[:, 0:32], T.dg[:, :], T.f2[:, :], False, False),
           mat(T.psv[:, 0:32], T.dg[:, :], T.f1[:, :], False, False, [f1]),
           mat(T.psv[:, 0:32], T.sg[:, :], T.s2[:, :], False, True, [sg, s2])]
-    mask = [act(T.mask[:, at:at + hi - lo], bank[:, 0:hi - lo], F.Copy, bias=S + UP, scale=-1.0, deps=[psw[h]])
-            for h, (bank, lo, hi, at) in enumerate(banks)]
-    wf = act(T.win[:, G0:G0 + FILL], T.mask[:, 0:FILL], F.Copy, scale=0.0, deps=mask)
+    plane(T.psa, 0, 128, 256, False)
+    mask.append(masks(T.psa, 0, J - 32, plane(T.psa, 0, 256, J, True)))
     p2 = [mat(T.ps2[:, 0:33], T.lt[:, :], T.f0[:, :], True, False, [f0, fe]),
           mat(T.ps2[:, 0:c], T.dg[:, :], T.f0[:, 0:c], False, False),
           mat(T.ps2[:, c:33], T.dgn[:, :], T.f0[:, c:33], False, False, [dgn]),
           mat(T.ps2[:, 0:33], T.sg[:, :], T.sm[:, :], False, True, [sm]),
           mat(T.ps2[:, 40:41], T.sg[:, :], T.sm[:, c - 1:c], True, True)]
+    if later:
+        mat(T.psh[:, 0:15], T.dg[:, :], T.step[:, 0:15], True, False)
+        mat(T.psh[:, 0:15], T.sel3[0:32, :], T.mi[0:32, 1:16], False, False)
+    p4 = act(T.p4[:, :], T.pan[:, :], F.Copy, bias=516.0 + 129.0 - 0.375, scale=0.25, deps=[pan])
+    wf = act(T.win[:, G0:G0 + FILL], T.mask[:, 0:FILL], F.Copy, scale=0.0, deps=mask)
+    qn = act(T.qn[:, :], T.p4[:, :], F.Identity, bias=T.pan[:, :], scale=-4.0, deps=[p4])
+    u4 = act(T.u4[:, :], T.qn[:, :], F.Relu, bias=12.0 * 2578, scale=12.0, deps=[qn])
 
     offv = ts(T.offv[:, :], T.psv[:, 0:32], T.kcol[:, :], A.add, 528.0, A.min, pv)
-    offa = ts(T.offa[:, 0:c], T.ps2[:, 0:c], T.ps2[:, 40:41], A.subtract, T.acol[:, :], A.add, p2 + [acol])
-    ends = [(T.offb, c, 32), (T.offc, 32, 33)] if later else [(T.offb, c, 33)]
-    offb = [ts(o[:, 0:hi - lo], T.ps2[:, lo:hi], T.ps2[:, 40:41], A.subtract, T.kcol[:, :], A.subtract) for o, lo, hi in ends]
     if r:
         vh = ts(T.vh[:, :], T.vw[:, :].indirect(T.offv[:, 0:1]), S + UP, A.add, deps=[l_val, offv] + vn)
         send(r - 1, T.vx[:, :], T.vh[:, :], "tv", [vh])
-    if later:
-        after("g", [sm, l_val])
-        ids = [DstId(rid=rid, pnc=pnc) for rid, pnc in (topo.addr(T.cores[d], core) for d in later)]
-        g.remote_dma_fused([RemoteDMATransfer(dst_ids=ids, dma_engine_mask=topo.mask(core, T.cores[later[0]]),
-                                              remote_sem=T.sem["m%d" % r], srcs=[T.sm[:, 16:32]],
-                                              dsts=[T["msg%d" % r][:, :] for d in later])], local_sem=T.sem["loc"])
-        sent[0] += len(topo.engines(core, T.cores[later[0]]))
-    mm = [tt(T.mm[:, at:at + hi - lo], T.vw[:, :].indirect(T.offv[:, lo // 16:hi // 16]), T.mask[:, at:at + hi - lo], A.add,
-             [l_val, offv, mask[h]] + vn) for h, (bank, lo, hi, at) in enumerate(banks)]
-    va = scan(T.va[:, 1:J + 1], T.psa[:, 0:J], T.mm[:, 0:J], 0.0, A.max, A.min, [mm[0]])
+
+    def gather(lo, hi, deps):
+        return tt(T.mm[:, lo:hi], T.vw[:, :].indirect(T.offv[:, lo // 16:hi // 16]), T.mask[:, lo:hi], A.add, deps)
+    mb = gather(J - 32, 512, [l_val, offv, mask[0]] + vn)
+    ma = gather(0, J - 32, [mask[1]])
+    vb = scan(T.vb[:, 1:K + 1], T.psb[:, 16:K + 16], T.mm[:, J - 16:512], 0.0, A.max, A.min, [mb])
+    offa = ts(T.offa[:, 0:c], T.ps2[:, 0:c], T.ps2[:, 40:41], A.subtract, T.acol[:, :], A.add, p2 + [acol])
+    offb = ts(T.offb[:, 0:33 - c], T.ps2[:, c:33], T.ps2[:, 40:41], A.subtract, T.kcol[:, :], A.subtract)
+    va = scan(T.va[:, 1:J + 1], T.psa[:, 0:J], T.mm[:, 0:J], 0.0, A.max, A.min, [ma])
     sa = do("s", lambda e: e.activation(T.win[:, 0:Z].indirect(T.offa[:, 0:c]), T.va[:, 0:J], F.Silu), [offa, va, wf] + v0)
-    vb = scan(T.vb[:, 1:K + 1], T.psb[:, 0:K], T.mm[:, J:J + K], 0.0, A.max, A.min, [mm[1]])
     if later:
         hp = scan(T.hp[0:64, :], T.hx[0:64, 0:16], T.hx[0:64, 16:32], T.cp[0:64, 143:144], A.add, A.min, [landed("ta", r + 1)])
         psh = mat(T.psh[:, 0:15], T.sel3[0:64, :], T.hp[0:64, 0:15], False, True, [hp])
@@ -216,34 +241,35 @@ def rank_program(g, core, T, topo):
     for p in range(r):
         pt.append(mat(T.pst[:, 0:1], T.sg[:, :], T["msg%d" % p][:, 15:16], False, p == r - 1, [landed("m%d" % p, p)]))
 
-    def scatter(offsets, lo, hi, deps=(), at=16):
-        return do("v", lambda e: e.tensor_copy(T.win[:, Z:Z + 17 * W].indirect(offsets[:, lo:hi]),
-                                               T.vb[:, at + 16 * lo:at + 16 * hi]), deps)
-    sv = [scatter(T.offb, 0, (32 if later else 33) - c, offb + [vb, wf] + v0)]
+    def scatter(lo, hi, deps):
+        return do("v", lambda e: e.tensor_copy(T.win[:, Z:Z + 17 * W].indirect(T.offb[:, lo:hi]),
+                                               T.vb[:, 16 + 16 * lo:16 + 16 * hi]), deps)
+    sv = [scatter(0, (32 if later else 33) - c, [offb, vb, wf] + v0)]
     if later:
         mh = tt(T.mh[:, 0:15], T.vx[:, 0:15], T.psh[:, 0:15], A.subtract, [psh, landed("tv", r + 1)])
+        vc = scan(T.vb[:, K + 1:K + 16], T.psh[:, 0:15], T.mh[:, 0:15], T.vb[:, K:K + 1], A.max, A.min, [mh])
     lst = ts(T.lst[:, :], T.tn[:, :], T.pst[:, 0:1], A.subtract, FILL - 1.0, A.min, pt + tn)
     if later:
-        vc = scan(T.vb[:, K + 1:K + 16], T.psh[:, 0:15], T.mh[:, 0:15], T.vb[:, K:K + 1], A.max, A.min, [mh])
-        sv.append(scatter(T.offc, 0, 1, [vc] + sv, K))
+        sv.append(scatter(32 - c, 33 - c, [vc] + sv))
 
     def pick(lo, hi):
         return T.win[:, G0:G0 + FILL].indirect(T.lst[:, lo:hi])
     ready = [sa, lst] + sv
-    b1 = ts(T.out1[:, :], pick(0, 7), -UP, A.add, deps=ready)
-    b3 = act(T.out3[:, :], pick(16, 24), F.Copy, bias=-UP, deps=ready)
+    b1 = [ts(T.out1[:, 0:64], pick(0, 4), -UP, A.add, deps=ready),
+          act(T.out1[:, 64:112], pick(4, 7), F.Copy, bias=-UP, deps=ready)]
+    b3 = act(T.out3[:, :], pick(16, 24), F.Copy, bias=-UP)
     b2 = ts(T.out2[:, :], pick(8, 15), -UP, A.add)
-    b3 = [turn(T.turned[:, b, :], T.out3[:, b::4], [b3]) for b in range(4)]
     own = ts(T.acc[:, :], pick(24, 32), -UP, A.add, -2.0, A.max)
-    send(dest[1], T.in1[:, :], T.out1[:, 0:BLK], "h1", [b1])
+    b3 = [turn(T.turned[:, b, :], T.out3[:, b::4], [b3]) for b in range(4)]
+    send(dest[1], T.in1[:, :], T.out1[:, 0:BLK], "h1", b1)
     send(dest[2], T.in2[:, :], T.out2[:, 0:BLK], "h2", [b2])
     send(dest[3], T.in3[:, :, :], T.turned[:, :, :], "h3", b3)
-    m = own
-    for k in (1, 2):
-        p = (r - k) % N
-        part = T.acc[:, 8 * p:8 * p + BLK]
-        m = tt(part, part, T["in%d" % k][:, :], A.max, [m, landed("h%d" % k, p)])
-    ta = [turn(T.ta[:, b, :], T.acc[:, b::4], [m]) for b in range(4)]
+    p, q = (r - 1) % N, (r - 2) % N
+    part = T.acc[:, 8 * p:8 * p + BLK]
+    m1 = tt(part, part, T.in1[:, :], A.max, [own, landed("h1", p)])
+    parts = [T.acc[:, 8 * q + b:8 * q + BLK:4] for b in range(4)]
+    m = [tt(parts[b], parts[b], T.in2[:, b::4], A.max, [m1, landed("h2", q)]) for b in range(4)]
+    ta = [turn(T.ta[:, b, :], T.acc[:, b::4], [m[b]]) for b in range(4)]
     for h, q in enumerate("ys"):
         fin = tt(T.fin[:, h, :, :], T.ta[:, 0:4, 16 * h:16 * h + 16], T.in3[:, :, 16 * h:16 * h + 16], A.max,
                  ta + [landed("h3", (r - 3) % N)])

from concourse.bass import DstId, RemoteDMATransfer
from concourse.mybir import AluOpType as A, ActivationFunctionType as F

H = 26
BLK = 4 * H
J = 320
K = 512 - J + 16
W = 512
LOW = J + 8
FILL = LOW + 512 - J + 8
G0, Z = 16 * W, 16 * W + LOW
S, UP = float(1 << 22), 64.0
I32, F32, B16, U16 = "int32", "float32", "bfloat16", "uint16"


def sb(width, dtype):
    return ("sbuf", [128] + (width if isinstance(width, list) else [width]), dtype)


SCRATCH = {
    "lt0": sb(64, I32), "lw": sb(64, I32), "rlc": sb(144, I32), "vw": sb(544, I32),
    "f0": sb(33, B16), "sm": sb(33, B16), "f1": sb(32, B16), "f2": sb(32, B16), "s2": sb(32, B16),
    "offv": sb(32, U16), "offa": sb(32, U16), "offb": sb(32, U16), "offc": sb(2, U16), "lst": sb(32, U16), "tn": sb(32, F32),
    "ca": sb(144, B16), "cb": sb(144, B16), "cp": sb(144, B16),
    "hm": sb(32, B16), "hx": sb(32, B16), "vh": sb(16, F32), "vx": sb(16, F32), "hp": sb(16, B16), "mh": sb(16, F32),
    "mask": sb(528, B16), "mm": sb(528, F32), "va": sb(J + 1, F32), "vb": sb(K + 16, F32), "win": sb(Z + 17 * W, F32),
    "msg0": sb(16, B16), "msg1": sb(16, B16), "msg2": sb(16, B16),
    "out1": sb(112, F32), "out2": sb(112, F32), "out3": sb(128, F32), "turned": sb([4, 32], F32),
    "in1": sb(BLK, F32), "in2": sb(BLK, F32), "in3": sb([4, 32], F32),
    "acc": sb(128, F32), "ta": ("psum", [128, 16, 32], F32), "fin": sb([2, 4, 16], F32),
    "mi": sb(128, B16), "mg": sb(128, B16), "mgk": sb(128, B16), "sg": sb(128, B16), "lt": sb(128, B16),
    "dg": sb(128, B16), "dgn": sb(128, B16), "step": sb(J, B16),
    "sel0": sb(128, B16), "sel1": sb(128, B16), "sel2": sb(128, B16), "sel3": sb(128, B16),
    "pin": sb(1, F32), "pw": sb(1, F32), "kgb": sb(1, B16), "pan": sb(1, F32), "kmod": sb(1, F32), "ccol": sb(1, F32),
    "kcol": sb(1, F32), "acol": sb(1, F32), "p4": sb(1, B16), "qn": sb(1, F32), "u4": sb(1, B16),
    "hs": sb(1, F32), "hc": sb(1, F32),
}
for _b in ("ps2", "pst", "psv", "psh", "psa", "psb"):
    SCRATCH[_b] = ("psum", [128, 512], "float32")
SEMAPHORES = ["s%d" % i for i in range(120)] + ["m0", "m1", "m2", "ta", "tv", "h1", "h2", "h3", "loc"]


def rank_program(g, core, T, topo):
    r = T.rank_of(core)
    if r is None:
        return
    N = len(T.cores)
    queues = {"g": g, "v": g.vector, "s": g.scalar, "p": g.tensor, "y": g.sync}
    seen = {q: [] for q in queues}
    used = []
    sent = [0]

    def after(q, deps):
        for d in deps:
            if d not in seen[q]:
                queues[q].wait_ge(T.sem[d[0]], d[1])
                seen[q].append(d)

    def new():
        used.append("s%d" % len(used))
        return used[-1]

    def do(q, call, deps=()):
        after(q, deps)
        n = new()
        call(queues[q]).then_inc(T.sem[n], 1)
        return (n, 1)

    def load(parts):
        n = new()
        for q, out, in_ in parts:
            queues[q].dma_start(out, in_).then_inc(T.sem[n], 16)
        return (n, 16 * len(parts))

    def fill(out, x):
        return do("v", lambda e: e.memset(out, x))

    def ts(out, in0, s1, op0, s2=None, op1=None, deps=()):
        if op1 is None:
            return do("v", lambda e: e.tensor_scalar(out, in0, s1, None, op0), deps)
        return do("v", lambda e: e.tensor_scalar(out, in0, s1, s2, op0, op1), deps)

    def scan(out, x0, x1, initial, op0, op1, deps=()):
        return do("v", lambda e: e.tensor_tensor_scan(out, x0, x1, initial, op0, op1), deps)

    def tt(out, in0, in1, op, deps=()):
        return do("v", lambda e: e.tensor_tensor(out, in0, in1, op), deps)

    def turn(out, in_, deps=()):
        return do("v", lambda e: e.transpose(out, in_), deps)

    def mat(out, lhs, rhs, start, stop, deps=()):
        return do("p", lambda e: e.matmul(out, lhs, rhs, start, stop), deps)

    def act(out, in_, func, bias=0.0, scale=1.0, deps=()):
        return do("s", lambda e: e.activation(out, in_, func, bias=bias, scale=scale), deps)

    def iota(out, pattern, base, per_partition):
        return do("g", lambda e: e.iota(out, pattern, base, per_partition, allow_small_or_imprecise_dtypes=True))

    def send(d, out, in_, sem, deps):
        after("g", deps)
        rid, pnc = topo.addr(T.cores[d], core)
        g.remote_dma(out, in_, T.sem[sem], T.sem["loc"], pnc, rid, topo.mask(core, T.cores[d]))
        sent[0] += len(topo.engines(core, T.cores[d]))

    def landed(sem, p):
        return (sem, len(topo.engines(T.cores[p], core)))

    def counts(to, deps):
        after("g", deps)
        ids = [DstId(rid=rid, pnc=pnc) for rid, pnc in (topo.addr(T.cores[d], core) for d in to)]
        g.remote_dma_fused([RemoteDMATransfer(dst_ids=ids, dma_engine_mask=topo.mask(core, T.cores[to[0]]),
                                              remote_sem=T.sem["m%d" % r], srcs=[T.sm[:, 16:32]],
                                              dsts=[T["msg%d" % r][:, :] for d in to])], local_sem=T.sem["loc"])
        sent[0] += len(topo.engines(core, T.cores[to[0]]))

    blk = [(a - r) % 4 for a in range(4)]
    later = [d for d in range(r + 1, N)]
    dest = [(r + k) % N for k in range(N)]
    c = J // 16

    def lists(x, at):
        return load([(q, T.lt0[:, at + 16 * h:at + 16 * h + 16], x[h::2, :]) for h, q in enumerate("ys")])
    parts = []
    for a in range(4):
        for q, row in (("y", 8 * blk[a]), ("s", 32 + 8 * blk[a])):
            lo = max(0, 128 * a - 16)
            parts.append((q, T.rlc[row:row + 8, :], T.rl[:, lo:lo + 144]))
    l_rlc = load(parts)
    l_lst = [lists(T.rl, 0), lists(T.dl, 32)]
    l_val = load([("sy"[w > 5], T.vw[w::16, 16:528], T.val[:, :]) for w in range(16)])

    pin = iota(T.pin[:, :], [[0, 1]], 0, 1)
    mg = iota(T.mg[:, :], [[1, 8], [0, 16]], 129, 0)
    mi = iota(T.mi[:, :], [[1, 128]], 0, 0)
    tn = [iota(T.tn[:, 16 * i:16 * i + 16], [[4 * (d1 - d0), 2], [64, 8]], LOW + 1 + 2064 + 48 + 4 * d0 + first, 1)
          for i, (d0, d1, first) in enumerate(((dest[1], dest[2], 32 * r), (dest[3], r, 0)))]
    cc = [fill(T.ccol[32 * i:32 * i + 32, :], 2.0 + i / 4) for i in range(2)]
    vn = [fill(T.vw[:, 0:16], -2), fill(T.vw[:, 528:544], -1)]
    v0 = [fill(T.va[:, 0:1], 0.0)] + ([] if later else [fill(T.vb[:, K + 1:K + 16], 0.0)])
    step = fill(T.step[:, :], -S / W)
    kgb = ts(T.kgb[:, :], T.pin[:, :], 1.0 / 16, A.mult, 129.0 - 7.5 / 16, A.add, [pin])
    pw = ts(T.pw[:, :], T.pin[:, :], 2065.0, A.add, -float(W), A.mult)
    km = ts(T.kmod[0:64, :], T.ccol[0:64, :], 128.0, A.mult, T.pin[0:64, :], A.subtract, cc)
    if r:
        hz = fill(T.hm[64:128, :], 0.0)
        hs = ts(T.hs[0:64, :], T.ccol[0:64, :], 3.125, A.mult, -7.0, A.add)
        hc = ts(T.hc[0:64, :], T.ccol[0:64, :], 409.0, A.mult, -918.0, A.add)
    kcol = ts(T.kcol[:, :], T.kgb[:, :], 16.0 * W, A.mult, T.pw[:, :], A.add, [kgb, pw])
    mgk = ts(T.mgk[0:64, :], T.mg[0:64, :], T.kmod[0:64, :], A.add, -256.0, A.add, [mg, km])
    sg = ts(T.sg[:, :], T.mg[:, :], T.kgb[:, :], A.is_equal)
    lt = do("g", lambda e: e.affine_select(T.lt[:, :], T.sg[:, :], [[-1, 128]], A.is_ge, 0.0, 0, 1), [sg])
    pan = ts(T.pan[:, :], T.kgb[:, :], -16.0, A.mult, T.pin[:, :], A.add)
    dg = ts(T.dg[:, :], T.mi[:, :], T.pin[:, :], A.is_equal, T.kcol[:, :], A.mult, [kcol, mi])
    acol = act(T.acol[:, :], T.kcol[:, :], F.Silu, bias=float(Z), deps=[kcol])
    for bank, n in [(T.psb, K + 32), (T.psa, J)]:
        mat(bank[:, 0:n], T.dg[:, :], T.step[:, 0:n], True, False, [dg, step])

    def select(a):
        return ts(T["sel%d" % a][0:64, :], T.mgk[0:64, :], 129.0 - 8 * blk[a], A.is_equal, -16 * S, A.mult, [mgk])
    sel = {a: select(a) for a in (2, 3)}

    if r:
        ha = ts(T.hm[0:64, 0:16], T.rlc[0:64, 0:16], T.hs[0:64, :], A.mult, -1.0, A.max, [hs, l_rlc])
        hb = ts(T.hm[0:64, 16:32], T.rlc[0:64, 0:16], T.hc[0:64, :], A.subtract, -1.125, A.is_ge, [hc])
        send(r - 1, T.hx[:, :], T.hm[:, :], "ta", [hz, ha, hb])
    calls = {
        "ca": lambda: ts(T.ca[0:64, :], T.rlc[0:64, :], T.ccol[0:64, :], A.subtract, -0.25, A.mult, [l_rlc]),
        "cb": lambda: ts(T.cb[0:64, :], T.rlc[0:64, :], T.ccol[0:64, :], A.subtract, -1.125, A.is_ge, [l_rlc]),
        "cp": lambda: scan(T.cp[0:64, :], T.ca[0:64, :], T.cb[0:64, :], 1.0, A.add, A.min, [made["ca"], made["cb"]]),
        "dgn": lambda: ts(T.dgn[:, :], T.dg[:, :], -1.0, A.mult, deps=[dg]),
        "lw0": lambda: turn(T.lw[:, 0:32], T.lt0[:, 0:32], [l_lst[0]]),
        "lw2": lambda: turn(T.lw[:, 32:64], T.lt0[:, 32:64], [l_lst[1]]),
        "f0": lambda: ts(T.f0[:, 0:32], T.lw[:, 0:32], 0.0, A.is_equal, -1.0, A.mult, [made["lw0"]]),
        "f1": lambda: ts(T.f1[:, :], T.lw[:, 32:64], 1.0, A.is_equal, -2.0, A.mult, [made["lw2"]]),
        "f2": lambda: ts(T.f2[:, :], T.lw[:, 32:64], 2.0, A.is_equal, -1.0, A.mult, [made["lw2"]]),
        "sm": lambda: scan(T.sm[:, :], T.f0[:, :], T.f0[:, :], 0.0, A.max, A.subtract, [made["f0"], made["fe"]]),
        "fe": lambda: ts(T.f0[:, 32:33], T.pan[:, :], (15 if later else 0) - 2064.0, A.is_equal, -1.0, A.mult, [pan]),
        "sel0": lambda: select(0),
        "sel1": lambda: select(1),
        "s2": lambda: scan(T.s2[:, :], T.f2[:, :], T.f2[:, :], 1.0, A.max, A.subtract, [made["f2"]]),
    }
    made = {}
    for name in "ca cb lw0 sel0 fe lw2 cp f0 sel1 f2 f1 sm dgn s2".split():
        made[name] = calls[name]()
    cp, dgn, fe, f0, f1, f2, sm, s2 = (made[name] for name in "cp dgn fe f0 f1 f2 sm s2".split())
    sel.update({0: made["sel0"], 1: made["sel1"]})
    if later:
        counts(later, [sm, s2])

    def plane(bank, lo, x0, x1, stop):
        a = x0 // 128
        at = x0 - 128 * a + (16 if a else 0)
        return mat(bank[:, x0 - lo:x1 - lo], T["sel%d" % a][0:64, :], T.cp[0:64, at:at + x1 - x0], False, stop, [sel[a], cp])

    def masks(bank, lo, end, last):
        return act(T.mask[:, lo:end], bank[:, 0:end - lo], F.Copy, bias=S + UP, scale=-1.0, deps=[last])
    plane(T.psb, J - 32, J - 32, 384, False)
    mask = [masks(T.psb, J - 32, 528, plane(T.psb, J - 32, 384, 512, True))]
    plane(T.psa, 0, 0, 128, False)
    pv = [mat(T.psv[:, 0:32], T.lt[:, :], T.f2[:, :], True, False, [lt, f2]),
          mat(T.psv[:, 0:32], T.dg[:, :], T.f2[:, :], False, False),
          mat(T.psv[:, 0:32], T.dg[:, :], T.f1[:, :], False, False, [f1]),
          mat(T.psv[:, 0:32], T.sg[:, :], T.s2[:, :], False, True, [sg, s2])]
    plane(T.psa, 0, 128, 256, False)
    mask.append(masks(T.psa, 0, J - 32, plane(T.psa, 0, 256, J, True)))
    p2 = [mat(T.ps2[:, 0:33], T.lt[:, :], T.f0[:, :], True, False, [f0, fe]),
          mat(T.ps2[:, 0:c], T.dg[:, :], T.f0[:, 0:c], False, False),
          mat(T.ps2[:, c:33], T.dgn[:, :], T.f0[:, c:33], False, False, [dgn]),
          mat(T.ps2[:, 0:33], T.sg[:, :], T.sm[:, :], False, True, [sm]),
          mat(T.ps2[:, 40:41], T.sg[:, :], T.sm[:, c - 1:c], True, True)]
    if later:
        mat(T.psh[:, 0:15], T.dg[:, :], T.step[:, 0:15], True, False)
        mat(T.psh[:, 0:15], T.sel3[0:32, :], T.mi[0:32, 1:16], False, False)
    p4 = act(T.p4[:, :], T.pan[:, :], F.Copy, bias=516.0 + 129.0 - 0.375, scale=0.25, deps=[pan])
    wf = act(T.win[:, G0:G0 + FILL], T.mask[:, 0:FILL], F.Copy, scale=0.0, deps=mask)
    qn = act(T.qn[:, :], T.p4[:, :], F.Identity, bias=T.pan[:, :], scale=-4.0, deps=[p4])
    u4 = act(T.u4[:, :], T.qn[:, :], F.Relu, bias=12.0 * 2578, scale=12.0, deps=[qn])

    offv = ts(T.offv[:, :], T.psv[:, 0:32], T.kcol[:, :], A.add, 528.0, A.min, pv)
    if r:
        vh = ts(T.vh[:, :], T.vw[:, :].indirect(T.offv[:, 0:1]), S + UP, A.add, deps=[l_val, offv] + vn)
        send(r - 1, T.vx[:, :], T.vh[:, :], "tv", [vh])

    def gather(lo, hi, deps):
        return tt(T.mm[:, lo:hi], T.vw[:, :].indirect(T.offv[:, lo // 16:hi // 16]), T.mask[:, lo:hi], A.add, deps)
    mb = gather(J - 32, 512, [l_val, offv, mask[0]] + vn)
    ma = gather(0, J - 32, [mask[1]])
    vb = scan(T.vb[:, 1:K + 1], T.psb[:, 16:K + 16], T.mm[:, J - 16:512], 0.0, A.max, A.min, [mb])
    offa = ts(T.offa[:, 0:c], T.ps2[:, 0:c], T.ps2[:, 40:41], A.subtract, T.acol[:, :], A.add, p2 + [acol])
    offb = ts(T.offb[:, 0:33 - c], T.ps2[:, c:33], T.ps2[:, 40:41], A.subtract, T.kcol[:, :], A.subtract)
    va = scan(T.va[:, 1:J + 1], T.psa[:, 0:J], T.mm[:, 0:J], 0.0, A.max, A.min, [ma])
    sa = do("s", lambda e: e.activation(T.win[:, 0:Z].indirect(T.offa[:, 0:c]), T.va[:, 0:J], F.Silu), [offa, va, wf] + v0)
    if later:
        hp = scan(T.hp[0:64, :], T.hx[0:64, 0:16], T.hx[0:64, 16:32], T.cp[0:64, 143:144], A.add, A.min, [landed("ta", r + 1)])
        psh = mat(T.psh[:, 0:15], T.sel3[0:64, :], T.hp[0:64, 0:15], False, True, [hp])
    pt = [mat(T.pst[:, 0:1], T.sg[:, :], T.sm[:, c - 1:c], True, False),
          mat(T.pst[:, 0:1], T.sg[:, :], T.kgb[:, :], False, False),
          mat(T.pst[:, 0:1], T.lt[:, :], T.u4[:, :], False, not r, [u4])]
    for p in range(r):
        pt.append(mat(T.pst[:, 0:1], T.sg[:, :], T["msg%d" % p][:, 15:16], False, p == r - 1, [landed("m%d" % p, p)]))

    def scatter(lo, hi, deps):
        return do("v", lambda e: e.tensor_copy(T.win[:, Z:Z + 17 * W].indirect(T.offb[:, lo:hi]),
                                               T.vb[:, 16 + 16 * lo:16 + 16 * hi]), deps)
    sv = [scatter(0, (32 if later else 33) - c, [offb, vb, wf] + v0)]
    if later:
        mh = tt(T.mh[:, 0:15], T.vx[:, 0:15], T.psh[:, 0:15], A.subtract, [psh, landed("tv", r + 1)])
        vc = scan(T.vb[:, K + 1:K + 16], T.psh[:, 0:15], T.mh[:, 0:15], T.vb[:, K:K + 1], A.max, A.min, [mh])
    lst = ts(T.lst[:, :], T.tn[:, :], T.pst[:, 0:1], A.subtract, FILL - 1.0, A.min, pt + tn)
    if later:
        sv.append(scatter(32 - c, 33 - c, [vc] + sv))

    def pick(lo, hi):
        return T.win[:, G0:G0 + FILL].indirect(T.lst[:, lo:hi])
    ready = [sa, lst] + sv
    b1 = [ts(T.out1[:, 0:64], pick(0, 4), -UP, A.add, deps=ready),
          act(T.out1[:, 64:112], pick(4, 7), F.Copy, bias=-UP, deps=ready)]
    b3 = act(T.out3[:, :], pick(16, 24), F.Copy, bias=-UP)
    b2 = ts(T.out2[:, :], pick(8, 15), -UP, A.add)
    own = ts(T.acc[:, :], pick(24, 32), -UP, A.add, -2.0, A.max)
    b3 = [turn(T.turned[:, b, :], T.out3[:, b::4], [b3]) for b in range(4)]
    send(dest[1], T.in1[:, :], T.out1[:, 0:BLK], "h1", b1)
    send(dest[2], T.in2[:, :], T.out2[:, 0:BLK], "h2", [b2])
    send(dest[3], T.in3[:, :, :], T.turned[:, :, :], "h3", b3)
    p, q = (r - 1) % N, (r - 2) % N
    part = T.acc[:, 8 * p:8 * p + BLK]
    m1 = tt(part, part, T.in1[:, :], A.max, [own, landed("h1", p)])
    parts = [T.acc[:, 8 * q + b:8 * q + BLK:4] for b in range(4)]
    m = [tt(parts[b], parts[b], T.in2[:, b::4], A.max, [m1, landed("h2", q)]) for b in range(4)]
    ta = [turn(T.ta[:, b, :], T.acc[:, b::4], [m[b]]) for b in range(4)]
    for h, q in enumerate("ys"):
        fin = tt(T.fin[:, h, :, :], T.ta[:, 0:4, 16 * h:16 * h + 16], T.in3[:, :, 16 * h:16 * h + 16], A.max,
                 ta + [landed("h3", (r - 3) % N)])
        after(q, [fin])
        n = new()
        queues[q].dma_start(T.y[h::2, :], T.fin[:, h, :, :]).then_inc(T.sem[n], 16)
        after(q, [(n, 16)])

    g.wait_ge(T.sem["loc"], sent[0])
    waited = [d[0] for q in seen for d in seen[q]]
    for n in used:
        if n not in waited:
            g.wait_ge(T.sem[n], 1)
